import numpy as np
import ml_dtypes


def mxq(x, axis, fmt="e4m3"):
    dtype, down = {"e4m3": (ml_dtypes.float8_e4m3fn, 7), "e5m2": (ml_dtypes.float8_e5m2, 14)}[fmt]
    v = np.moveaxis(np.asarray(x, np.float32).astype(ml_dtypes.bfloat16).astype(np.float64), axis, -1)
    blocks = v.reshape(v.shape[:-1] + (-1, 32))
    amax = np.abs(blocks).max(-1, keepdims=True)
    byte = np.maximum(np.where(amax > 0, np.frexp(amax)[1] - 1 + 127, 0) - down, 1)
    scale = np.exp2(byte - 127.0)
    codes = (blocks / scale).astype(np.float32).astype(dtype).astype(np.float64)
    return np.moveaxis((codes * scale).reshape(v.shape), -1, axis)


WIDE = False


def mx_kscale(k):
    if not WIDE:
        return np.ones(k)
    levels = np.array([10, -10, 5, -5, 0])
    if k % 512:
        return np.exp2(np.random.permutation(np.resize(levels, k // 32))).repeat(32)
    a = np.empty((k // 512, 16))
    for p in range(k // 512):
        a[p, :8] = np.random.permutation(np.resize(levels, 8))
        for g in range(8):
            far = levels[np.abs(levels - a[p, g]) >= 10]
            a[p, g + 8] = far[np.random.randint(len(far))]
    return np.exp2(a.ravel()).repeat(32)


def f64(x):
    return np.asarray(x).astype(np.float64)


def striped(idx):
    return np.tile(idx.reshape(-1, 16).T, (8, 1)).astype(np.uint16)


def unstriped(offs):
    return offs[:16].T.reshape(-1).astype(np.int64)


E2M1 = np.array([0.0, 0.5, 1.0, 1.5, 2.0, 3.0, 4.0, 6.0, -0.0, -0.5, -1.0, -1.5, -2.0, -3.0, -4.0, -6.0])


def pack_weight(w, fmt):
    k, n = w.shape
    w = f64(np.asarray(w, np.float32).astype(ml_dtypes.bfloat16)).reshape(k // 32, 32, n)
    amax = np.abs(w).max(1)
    if fmt == "e4m3":
        byte = np.frexp(amax)[1] - 1 + 127 - 7
    else:
        mant, ex = np.frexp(amax / 6.0)
        byte = np.where(mant > 0.5, ex, ex - 1) + 127
    byte = np.clip(np.where(amax > 0, byte, 1), 1, 254)
    scaled = (w * np.exp2(127.0 - byte)[:, None, :]).reshape(k, n).astype(np.float32)
    by_word = np.ascontiguousarray(scaled.reshape(k // 512, 128, 4, n).transpose(0, 1, 3, 2))
    if fmt == "e4m3":
        words = by_word.astype(ml_dtypes.float8_e4m3fn).view(np.uint8)
    else:
        c = by_word.astype(ml_dtypes.float4_e2m1fn).view(np.uint8) & 0xF
        words = (c[..., 0::2] | (c[..., 1::2] << 4)).reshape(k // 512, 128, 2 * n)
    return np.ascontiguousarray(words), np.ascontiguousarray(byte.astype(np.uint8).reshape(k // 512, 16, n))


def unpack_weight(words, scales, fmt):
    g, _, n = scales.shape
    words = np.ascontiguousarray(words).reshape(g, 128, n, -1)
    if fmt == "e4m3":
        vals = words.view(ml_dtypes.float8_e4m3fn).astype(np.float64)
    else:
        nib = np.empty((g, 128, n, 4), np.uint8)
        nib[..., 0::2] = words & 0xF
        nib[..., 1::2] = words >> 4
        vals = E2M1[nib]
    vals = vals * np.repeat(np.exp2(scales.astype(np.float64) - 127.0), 8, axis=1)[..., None]
    return vals.transpose(0, 1, 3, 2).reshape(g * 512, n)


def gelu(v):
    return 0.5 * v * (1.0 + np.tanh(np.sqrt(2.0 / np.pi) * (v + 0.044715 * v**3)))


def pack_table4(v):
    words, scales = pack_weight(v, "e2m1")
    g, t = words.shape[0] // 2, v.shape[1]
    words = words.reshape(g, 2, 128, t, 2).transpose(0, 2, 3, 1, 4)
    return np.concatenate([words.reshape(g, -1), scales.reshape(g, -1)], axis=1)


def unpack_table4(tab):
    g, t = tab.shape[0], tab.shape[1] // 544
    words = tab[:, :512 * t].reshape(g, 128, t, 2, 2).transpose(0, 3, 1, 2, 4).reshape(2 * g, 128, 2 * t)
    return unpack_weight(words, tab[:, 512 * t:].reshape(2 * g, 16, t), "e2m1")


K, T, S, H, N = 1024, 4096, 1024, 1024, 512

def setup_inputs():
    n = np.random.standard_normal
    s = mx_kscale(K)[:, None]
    u = mx_kscale(H)[:, None]
    tab = pack_table4(n((K, T)) * s)
    offs = striped(np.random.permutation(T)[:S])
    w1 = n((K, H)) / np.sqrt(K) / s * u.T
    b1 = 0.5 * n(H) * u[:, 0]
    w2_words, w2_scales = pack_weight(n((H, N)) * np.sqrt(2.0 / H) / u, "e2m1")
    ws_words, ws_scales = pack_weight(n((K, N)) / np.sqrt(K) / s, "e4m3")
    b2 = 0.5 * n(N)
    ew = np.exp(0.3 * n(S))
    return {"tab": tab, "offs": offs,
            "w1": w1.astype(np.float32), "b1": b1.astype(np.float32),
            "w2_words": w2_words, "w2_scales": w2_scales,
            "ws_words": ws_words, "ws_scales": ws_scales,
            "b2": b2.astype(np.float32), "ew": ew.astype(np.float32)}

def reference(tab, offs, w1, b1, w2_words, w2_scales, ws_words, ws_scales, b2, ew):
    v = unpack_table4(tab)[:, unstriped(offs)]
    w1q = mxq(f64(w1), 0, "e4m3")
    w2 = unpack_weight(w2_words, w2_scales, "e2m1")
    ws = unpack_weight(ws_words, ws_scales, "e4m3")
    h = np.maximum((w1q.T @ v) + f64(b1)[:, None], 0.0)
    hq = mxq(h, 0, "e4m3")
    y = w2.T @ hq + ws.T @ v
    return (y + f64(b2)[:, None]) * f64(ew)[None, :]

@@ -1,0 +1,247 @@
+from contextlib import ExitStack
+
+import concourse.mybir as mybir
+
+K, T, S, H, N = 1024, 4096, 1024, 1024, 512
+FLOPS = 2 * S * (K * H + H * N + K * N)
+
+F32 = mybir.dt.float32
+BF16 = mybir.dt.bfloat16
+I32 = mybir.dt.int32
+U32 = mybir.dt.uint32
+U16 = mybir.dt.uint16
+U8 = mybir.dt.uint8
+FP8X4 = mybir.dt.float8_e4m3fn_x4
+FP4X4 = mybir.dt.float4_e2m1fn_x4
+ALU = mybir.AluOpType
+ACT = mybir.ActivationFunctionType
+
+P = 128
+HALF = 512
+V_SHARE = {(0, 0): 84, (0, 1): 84, (1, 0): 128, (1, 1): 84}
+
+
+def tile_list_edge_skip_messages_kernel(
+    tc, tab, offs, w1, b1, w2_words, w2_scales, ws_words, ws_scales, b2, ew, out
+):
+    nc = tc.nc
+    with ExitStack() as ctx:
+        keep = ctx.enter_context(tc.tile_pool(name="keep", bufs=1))
+        psum = ctx.enter_context(tc.psum_pool(name="psum", bufs=1))
+
+        def sb(name, shape, dtype, tag=None):
+            return keep.tile(shape, dtype, name=name, tag=tag or name, align_bytes=64)
+
+        def bank(b, name):
+            return psum.tile([P, HALF], F32, name=name, tag="bank%d" % b)
+
+        def w1_rows(a, g):
+            return w1[512 * g : 512 * (g + 1), 512 * a : 512 * (a + 1)].rearrange("(p j) c -> p j c", j=4)
+
+        def load_weight_scales(queue, plane, scales):
+            rows = plane[:].bitcast(I32).rearrange("p (a n) -> p a n", a=2)
+            for q in range(4):
+                queue.dma_start(
+                    out=rows[32 * q : 32 * q + 4],
+                    in_=scales[:, 4 * q : 4 * q + 4, :].rearrange("a r n -> r a n").bitcast(I32),
+                )
+
+        offsets = keep.tile([P, S // 16], U16, name="offsets")
+        nc.sync.dma_start(offsets[:], offs)
+
+        word_bytes = 512 * T
+        tab_scales = sb("tab_scales", [P, T], U8)
+        nc.sync.dma_start(
+            out=tab_scales[:].bitcast(I32)[0:32, :],
+            in_=tab[0, word_bytes:].rearrange("(i b) -> i b", i=32).bitcast(I32),
+        )
+        nc.vector.memset(tab_scales[:].bitcast(I32)[64:P, :], 0)
+        nc.vector.memset(tab_scales[:].bitcast(I32)[32:64, :], 0)
+        tab_words = sb("tab_words", [P, T], I32)
+        nc.sync.dma_start(out=tab_words[:], in_=tab[0, 0:word_bytes].rearrange("(p b) -> p b", p=P).bitcast(I32))
+        raw = {}
+        for g in range(2):
+            raw[0, g] = sb("raw0%d" % g, [P, 4, 512], F32)
+            nc.sync.dma_start(out=raw[0, g][:], in_=w1_rows(0, g))
+
+        b1_cols = sb("b1_cols", [P, 2, 4], F32)
+        nc.gpsimd.dma_start(out=b1_cols[:], in_=b1.rearrange("(a p t) -> p a t", a=2, t=4))
+        v_plane = [sb("v_plane%d" % g, [P, S], U8) for g in range(2)]
+        for g in range(2):
+            nc.gpsimd.memset(v_plane[g][:].bitcast(I32), 0)
+
+        picked_scales = sb("picked_scales", [P, S], U8)
+        nc.vector.tensor_copy(picked_scales[:], tab_scales[:].indirect(offsets[:]))
+        for g in range(2):
+            for q in range(4):
+                first = 16 * g + 4 * q
+                queue = nc.gpsimd if g == 1 and q >= 2 else nc.scalar
+                queue.dma_start(
+                    out=v_plane[g][:].bitcast(I32)[32 * q : 32 * q + 4, :],
+                    in_=picked_scales[:].bitcast(I32)[first : first + 4, :],
+                )
+        ws_plane = sb("ws_plane", [P, 2 * N], U8, tag="tab_scales")
+        nc.gpsimd.memset(ws_plane[:].bitcast(I32), 0)
+        load_weight_scales(nc.gpsimd, ws_plane, ws_scales)
+
+        v_codes = []
+        for half in range(2):
+            picked = sb("picked%d" % half, [P, HALF], U32)
+            nc.vector.tensor_copy(
+                picked[:], tab_words[:].bitcast(U32).indirect(offsets[:, 32 * half : 32 * (half + 1)])
+            )
+            parted = sb("v_codes%d" % half, [P, 4 * HALF], U8)
+            nc.vector.tensor_copy(
+                out=parted[:].bitcast(U16).rearrange("p (g n) -> p g n", g=2),
+                in_=picked[:].bitcast(U16).rearrange("p (n g) -> p g n", g=2),
+            )
+            v_codes.append(parted)
+
+        raw[1, 0] = sb("raw10", [P, 4, 512], F32, tag="picked0")
+        nc.sync.dma_start(out=raw[1, 0][:], in_=w1_rows(1, 0))
+        ws_codes = sb("ws_codes", [P, 2 * 4 * N], U8, tag="tab_words")
+        nc.sync.dma_start(
+            out=ws_codes[:].bitcast(I32).rearrange("p (a n) -> p a n", a=2),
+            in_=ws_words.rearrange("a p n t -> p a (n t)").bitcast(I32),
+        )
+        raw[1, 1] = sb("raw11", [P, 4, 512], F32, tag="picked1")
+        nc.sync.dma_start(out=raw[1, 1][:], in_=w1_rows(1, 1))
+
+        def v_operand(g, half):
+            codes = v_codes[half][:, 2 * HALF * g : 2 * HALF * (g + 1)].bitcast(FP4X4)
+            return codes, v_plane[g][:, HALF * half : HALF * (half + 1)]
+
+        w1_codes, w1_plane, grouped = {}, {}, {}
+
+        def round_w1(a, g):
+            grouped[a, g] = sb("grouped%d%d" % (a, g), [P, 2048], BF16)
+            dst = grouped[a, g][:].rearrange("p (t m j) -> p m j t", t=4, j=4)
+            src = raw[a, g][:].rearrange("p j (m t) -> p m j t", t=4)
+            share = V_SHARE[a, g]
+            nc.vector.tensor_copy(out=dst[:, 0:share], in_=src[:, 0:share])
+            if share < P:
+                nc.scalar.activation(out=dst[:, share:P], in_=src[:, share:P], func=ACT.Copy)
+
+        def quantize_w1(a, g):
+            w1_codes[a, g] = sb("w1_codes%d%d" % (a, g), [P, 512], U32)
+            w1_plane[a, g] = sb("w1_plane%d%d" % (a, g), [P, 512], U8)
+            nc.vector.quantize_mx(out=w1_codes[a, g][:].bitcast(FP8X4), scales=w1_plane[a, g][:], in_=grouped[a, g][:])
+
+        h_rows, h_codes, h_plane = {}, {}, {}
+
+        def first_layer(a, half):
+            h_rows[a, half] = sb("h_rows%d%d" % (a, half), [P, 4, HALF], BF16)
+            for t in range(4):
+                acc = bank(4 * half + t if a == 0 else (4 * half + t) % 3, "h_acc")
+                cols = slice(P * t, P * (t + 1))
+                for g in range(2):
+                    codes, plane = v_operand(g, half)
+                    nc.tensor.matmul_mx(
+                        out=acc[:],
+                        lhsT=w1_codes[a, g][:, cols].bitcast(FP8X4),
+                        lhsT_scale=w1_plane[a, g][:, cols],
+                        rhs=codes,
+                        rhs_scale=plane,
+                        start=(g == 0),
+                        stop=(g == 1),
+                    )
+                nc.scalar.activation(
+                    out=h_rows[a, half][:, t, :], in_=acc[:], func=ACT.Relu, bias=b1_cols[:, a, t : t + 1]
+                )
+
+        def quantize_h(a, half):
+            woven = sb("h_woven%d%d" % (a, half), [P, 4 * HALF], BF16)
+            nc.vector.tensor_copy(
+                out=woven[:].rearrange("p (c i t) -> p c t i", i=4, t=4),
+                in_=h_rows[a, half][:].rearrange("p t (c i) -> p c t i", i=4),
+            )
+            h_codes[a, half] = sb("h_codes%d%d" % (a, half), [P, HALF], U32)
+            h_plane[a, half] = sb("h_plane%d%d" % (a, half), [P, HALF], U8)
+            nc.vector.quantize_mx(out=h_codes[a, half][:].bitcast(FP8X4), scales=h_plane[a, half][:], in_=woven[:])
+
+        y_acc = {}
+
+        def skip_passes(m, half, b):
+            y_acc[m, half] = bank(b, "y_acc")
+            for g in range(2):
+                codes, plane = v_operand(g, half)
+                first = N * g + P * m
+                nc.tensor.matmul_mx(
+                    out=y_acc[m, half][:],
+                    lhsT=ws_codes[:, 4 * first : 4 * (first + P)].bitcast(FP8X4),
+                    lhsT_scale=ws_plane[:, first : first + P],
+                    rhs=codes,
+                    rhs_scale=plane,
+                    start=(g == 0),
+                    stop=False,
+                )
+
+        def second_layer(a, m, half):
+            first = N * a + P * m
+            nc.tensor.matmul_mx(
+                out=y_acc[m, half][:],
+                lhsT=w2_codes[:, 2 * first : 2 * (first + P)].bitcast(FP4X4),
+                lhsT_scale=w2_plane[:, first : first + P],
+                rhs=h_codes[a, half][:].bitcast(FP8X4),
+                rhs_scale=h_plane[a, half][:],
+                start=False,
+                stop=(a == 1),
+            )
+
+        def finish(m, half):
+            result = sb("result%d%d" % (m, half), [P, HALF], F32)
+            cols = slice(HALF * half, HALF * (half + 1))
+            nc.vector.scalar_tensor_tensor(
+                out=result[:], in0=y_acc[m, half][:], scalar=b2_cols[:, m : m + 1], in1=edge_weight[:, cols],
+                op0=ALU.add, op1=ALU.mult,
+            )
+            nc.sync.dma_start(out=out[P * m : P * (m + 1), cols], in_=result[:])
+
+        round_w1(0, 0)
+        quantize_w1(0, 0)
+        w2_codes = sb("w2_codes", [P, 2 * 2 * N], U8, tag="grouped00")
+        nc.sync.dma_start(
+            out=w2_codes[:].bitcast(I32).rearrange("p (a n) -> p a n", a=2),
+            in_=w2_words.rearrange("a p n -> p a n").bitcast(I32),
+        )
+        round_w1(0, 1)
+        quantize_w1(0, 1)
+        w2_plane = sb("w2_plane", [P, 2 * N], U8, tag="raw01")
+        nc.vector.memset(w2_plane[:].bitcast(I32), 0)
+        load_weight_scales(nc.sync, w2_plane, w2_scales)
+        b2_cols = sb("b2_cols", [P, 4], F32, tag="grouped01")
+        with nc.allow_non_contiguous_dma(reason="one bias value for each partition and row tile"):
+            nc.sync.dma_start(out=b2_cols[:], in_=b2.rearrange("(m p) -> p m", p=P))
+
+        first_layer(0, 0)
+        round_w1(1, 0)
+        quantize_w1(1, 0)
+        edge_weight = sb("edge_weight", [P, S], F32, tag="picked0")
+        for half in range(2):
+            cols = slice(HALF * half, HALF * (half + 1))
+            nc.sync.dma_start(out=edge_weight[:, cols], in_=ew[cols].partition_broadcast(P))
+        round_w1(1, 1)
+        quantize_w1(1, 1)
+        first_layer(0, 1)
+        quantize_h(0, 0)
+        first_layer(1, 0)
+        quantize_h(0, 1)
+        first_layer(1, 1)
+        for m in range(4):
+            skip_passes(m, 0, 3 + m)
+        skip_passes(0, 1, 7)
+        for m in range(4):
+            second_layer(0, m, 0)
+        second_layer(0, 0, 1)
+        quantize_h(1, 0)
+        for m in range(4):
+            second_layer(1, m, 0)
+        for m in range(1, 4):
+            skip_passes(m, 1, (m + 1) % 3)
+            second_layer(0, m, 1)
+        quantize_h(1, 1)
+        for m in range(4):
+            finish(m, 0)
+        for m in range(4):
+            second_layer(1, m, 1)
+            finish(m, 1)

@@ -18,7 +18,8 @@ ACT = mybir.ActivationFunctionType
 
 P = 128
 HALF = 512
-V_SHARE = {(0, 0): 84, (0, 1): 84, (1, 0): 128, (1, 1): 84}
+V_SHARE = {(0, 0): 64, (0, 1): 84, (1, 0): 128, (1, 1): 72}
+V_WEAVE_LAST = 344
 
 
 def tile_list_edge_skip_messages_kernel(
@@ -59,53 +60,78 @@ def tile_list_edge_skip_messages_kernel(
         nc.vector.memset(tab_scales[:].bitcast(I32)[32:64, :], 0)
         tab_words = sb("tab_words", [P, T], I32)
         nc.sync.dma_start(out=tab_words[:], in_=tab[0, 0:word_bytes].rearrange("(p b) -> p b", p=P).bitcast(I32))
-        raw = {}
-        for g in range(2):
-            raw[0, g] = sb("raw0%d" % g, [P, 4, 512], F32)
-            nc.sync.dma_start(out=raw[0, g][:], in_=w1_rows(0, g))
-
+        ws_plane = sb("ws_plane", [P, 2 * N], U8)
+        nc.gpsimd.memset(ws_plane[:].bitcast(I32), 0)
+        warm = sb("warm", [P, 2], F32)
+        nc.gpsimd.memset(warm[:, 0:1], 0.0)
+        nc.scalar.activation(out=warm[:, 1:2], in_=warm[:, 0:1], func=ACT.Relu)
+        load_weight_scales(nc.gpsimd, ws_plane, ws_scales)
         b1_cols = sb("b1_cols", [P, 2, 4], F32)
         nc.gpsimd.dma_start(out=b1_cols[:], in_=b1.rearrange("(a p t) -> p a t", a=2, t=4))
         v_plane = [sb("v_plane%d" % g, [P, S], U8) for g in range(2)]
-        for g in range(2):
-            nc.gpsimd.memset(v_plane[g][:].bitcast(I32), 0)
+        w2_plane = sb("w2_plane", [P, 2 * N], U8)
+        for plane in (v_plane[0], v_plane[1], w2_plane):
+            nc.vector.memset(plane[:].bitcast(I32), 0)
 
         picked_scales = sb("picked_scales", [P, S], U8)
         nc.vector.tensor_copy(picked_scales[:], tab_scales[:].indirect(offsets[:]))
-        for g in range(2):
+
+        def place_scale_rows(queue, g):
             for q in range(4):
                 first = 16 * g + 4 * q
-                queue = nc.gpsimd if g == 1 and q >= 2 else nc.scalar
                 queue.dma_start(
                     out=v_plane[g][:].bitcast(I32)[32 * q : 32 * q + 4, :],
                     in_=picked_scales[:].bitcast(I32)[first : first + 4, :],
                 )
-        ws_plane = sb("ws_plane", [P, 2 * N], U8, tag="tab_scales")
-        nc.gpsimd.memset(ws_plane[:].bitcast(I32), 0)
-        load_weight_scales(nc.gpsimd, ws_plane, ws_scales)
 
-        v_codes = []
-        for half in range(2):
-            picked = sb("picked%d" % half, [P, HALF], U32)
-            nc.vector.tensor_copy(
-                picked[:], tab_words[:].bitcast(U32).indirect(offsets[:, 32 * half : 32 * (half + 1)])
-            )
-            parted = sb("v_codes%d" % half, [P, 4 * HALF], U8)
-            nc.vector.tensor_copy(
-                out=parted[:].bitcast(U16).rearrange("p (g n) -> p g n", g=2),
-                in_=picked[:].bitcast(U16).rearrange("p (n g) -> p g n", g=2),
-            )
-            v_codes.append(parted)
+        raw, ws_codes = {}, {}
 
-        raw[1, 0] = sb("raw10", [P, 4, 512], F32, tag="picked0")
-        nc.sync.dma_start(out=raw[1, 0][:], in_=w1_rows(1, 0))
-        ws_codes = sb("ws_codes", [P, 2 * 4 * N], U8, tag="tab_words")
+        def load_w1(a, g):
+            raw[a, g] = sb("raw%d%d" % (a, g), [P, 4, 512], F32)
+            nc.sync.dma_start(out=raw[a, g][:], in_=w1_rows(a, g))
+
+        def load_ws(g):
+            ws_codes[g] = sb("ws_codes%d" % g, [P, 4 * N], U8)
+            nc.sync.dma_start(
+                out=ws_codes[g][:].bitcast(I32), in_=ws_words[g].rearrange("p n t -> p (n t)").bitcast(I32)
+            )
+
+        place_scale_rows(nc.scalar, 0)
+        load_ws(0)
+        load_w1(0, 0)
+        load_w1(0, 1)
+        place_scale_rows(nc.sync, 1)
+        load_w1(1, 0)
+        load_w1(1, 1)
+        load_ws(1)
+        w2_codes = sb("w2_codes", [P, 2 * 2 * N], U8)
         nc.sync.dma_start(
-            out=ws_codes[:].bitcast(I32).rearrange("p (a n) -> p a n", a=2),
-            in_=ws_words.rearrange("a p n t -> p a (n t)").bitcast(I32),
+            out=w2_codes[:].bitcast(I32).rearrange("p (a n) -> p a n", a=2),
+            in_=w2_words.rearrange("a p n -> p a n").bitcast(I32),
         )
-        raw[1, 1] = sb("raw11", [P, 4, 512], F32, tag="picked1")
-        nc.sync.dma_start(out=raw[1, 1][:], in_=w1_rows(1, 1))
+        load_weight_scales(nc.sync, w2_plane, w2_scales)
+        b2_cols = sb("b2_cols", [P, 4], F32)
+        with nc.allow_non_contiguous_dma(reason="one bias value for each partition and row tile"):
+            nc.sync.dma_start(out=b2_cols[:], in_=b2.rearrange("(m p) -> p m", p=P))
+        edge_weight = sb("edge_weight", [P, S], F32)
+        for half in range(2):
+            cols = slice(HALF * half, HALF * (half + 1))
+            nc.sync.dma_start(out=edge_weight[:, cols], in_=ew[cols].partition_broadcast(P))
+
+        picked, v_codes = {}, {}
+
+        def gather_words(half, tag):
+            picked[half] = sb("picked%d" % half, [P, HALF], U32, tag=tag)
+            nc.vector.tensor_copy(
+                picked[half][:], tab_words[:].bitcast(U32).indirect(offsets[:, 32 * half : 32 * (half + 1)])
+            )
+
+        def part_words(half):
+            v_codes[half] = sb("v_codes%d" % half, [P, 4 * HALF], U8)
+            nc.vector.tensor_copy(
+                out=v_codes[half][:].bitcast(U16).rearrange("p (g n) -> p g n", g=2),
+                in_=picked[half][:].bitcast(U16).rearrange("p (n g) -> p g n", g=2),
+            )
 
         def v_operand(g, half):
             codes = v_codes[half][:, 2 * HALF * g : 2 * HALF * (g + 1)].bitcast(FP4X4)
@@ -130,9 +156,11 @@ def tile_list_edge_skip_messages_kernel(
         h_rows, h_codes, h_plane = {}, {}, {}
 
         def first_layer(a, half):
-            h_rows[a, half] = sb("h_rows%d%d" % (a, half), [P, 4, HALF], BF16)
+            h_rows[a, half] = sb(
+                "h_rows%d%d" % (a, half), [P, 4, HALF], BF16, tag="raw11" if (a, half) == (0, 1) else None
+            )
             for t in range(4):
-                acc = bank(4 * half + t if a == 0 else (4 * half + t) % 3, "h_acc")
+                acc = bank(5 + (8 * a + 4 * half + t) % 3, "h_acc")
                 cols = slice(P * t, P * (t + 1))
                 for g in range(2):
                     codes, plane = v_operand(g, half)
@@ -150,31 +178,32 @@ def tile_list_edge_skip_messages_kernel(
                 )
 
         def quantize_h(a, half):
-            woven = sb("h_woven%d%d" % (a, half), [P, 4 * HALF], BF16)
-            nc.vector.tensor_copy(
-                out=woven[:].rearrange("p (c i t) -> p c t i", i=4, t=4),
-                in_=h_rows[a, half][:].rearrange("p t (c i) -> p c t i", i=4),
-            )
+            woven = sb("h_woven%d%d" % (a, half), [P, 4 * HALF], BF16, tag="grouped11" if (a, half) == (0, 0) else None)
+            dst = woven[:].rearrange("p (c i t) -> p c t i", i=4, t=4)
+            src = h_rows[a, half][:].rearrange("p t (c i) -> p c t i", i=4)
+            share = V_WEAVE_LAST // 4 if (a, half) == (1, 1) else P
+            nc.vector.tensor_copy(out=dst[:, 0:share], in_=src[:, 0:share])
+            if share < P:
+                nc.scalar.copy(out=dst[:, share:P], in_=src[:, share:P])
             h_codes[a, half] = sb("h_codes%d%d" % (a, half), [P, HALF], U32)
             h_plane[a, half] = sb("h_plane%d%d" % (a, half), [P, HALF], U8)
             nc.vector.quantize_mx(out=h_codes[a, half][:].bitcast(FP8X4), scales=h_plane[a, half][:], in_=woven[:])
 
         y_acc = {}
 
-        def skip_passes(m, half, b):
-            y_acc[m, half] = bank(b, "y_acc")
-            for g in range(2):
-                codes, plane = v_operand(g, half)
-                first = N * g + P * m
-                nc.tensor.matmul_mx(
-                    out=y_acc[m, half][:],
-                    lhsT=ws_codes[:, 4 * first : 4 * (first + P)].bitcast(FP8X4),
-                    lhsT_scale=ws_plane[:, first : first + P],
-                    rhs=codes,
-                    rhs_scale=plane,
-                    start=(g == 0),
-                    stop=False,
-                )
+        def skip_pass(g, m, half, b=None):
+            if g == 0:
+                y_acc[m, half] = bank(b, "y_acc")
+            codes, plane = v_operand(g, half)
+            nc.tensor.matmul_mx(
+                out=y_acc[m, half][:],
+                lhsT=ws_codes[g][:, 4 * P * m : 4 * P * (m + 1)].bitcast(FP8X4),
+                lhsT_scale=ws_plane[:, N * g + P * m : N * g + P * (m + 1)],
+                rhs=codes,
+                rhs_scale=plane,
+                start=(g == 0),
+                stop=False,
+            )
 
         def second_layer(a, m, half):
             first = N * a + P * m
@@ -188,60 +217,63 @@ def tile_list_edge_skip_messages_kernel(
                 stop=(a == 1),
             )
 
-        def finish(m, half):
+        def finish(m, half, pieces=1):
+            width = HALF // pieces
+            for i in range(pieces):
+                result = sb("result%d%d%d" % (m, half, i), [P, width], F32)
+                cols = slice(HALF * half + width * i, HALF * half + width * (i + 1))
+                nc.vector.scalar_tensor_tensor(
+                    out=result[:],
+                    in0=y_acc[m, half][:, width * i : width * (i + 1)],
+                    scalar=b2_cols[:, m : m + 1],
+                    in1=edge_weight[:, cols],
+                    op0=ALU.add,
+                    op1=ALU.mult,
+                )
+                nc.sync.dma_start(out=out[P * m : P * (m + 1), cols], in_=result[:])
+
+        def finish_aside(m, half, biased):
             result = sb("result%d%d" % (m, half), [P, HALF], F32)
             cols = slice(HALF * half, HALF * (half + 1))
-            nc.vector.scalar_tensor_tensor(
-                out=result[:], in0=y_acc[m, half][:], scalar=b2_cols[:, m : m + 1], in1=edge_weight[:, cols],
-                op0=ALU.add, op1=ALU.mult,
-            )
+            nc.scalar.activation(out=biased, in_=y_acc[m, half][:], func=ACT.Identity, bias=b2_cols[:, m : m + 1])
+            nc.gpsimd.tensor_tensor(out=result[:], in0=biased, in1=edge_weight[:, cols], op=ALU.mult)
             nc.sync.dma_start(out=out[P * m : P * (m + 1), cols], in_=result[:])
 
-        round_w1(0, 0)
-        quantize_w1(0, 0)
-        w2_codes = sb("w2_codes", [P, 2 * 2 * N], U8, tag="grouped00")
-        nc.sync.dma_start(
-            out=w2_codes[:].bitcast(I32).rearrange("p (a n) -> p a n", a=2),
-            in_=w2_words.rearrange("a p n -> p a n").bitcast(I32),
-        )
-        round_w1(0, 1)
-        quantize_w1(0, 1)
-        w2_plane = sb("w2_plane", [P, 2 * N], U8, tag="raw01")
-        nc.vector.memset(w2_plane[:].bitcast(I32), 0)
-        load_weight_scales(nc.sync, w2_plane, w2_scales)
-        b2_cols = sb("b2_cols", [P, 4], F32, tag="grouped01")
-        with nc.allow_non_contiguous_dma(reason="one bias value for each partition and row tile"):
-            nc.sync.dma_start(out=b2_cols[:], in_=b2.rearrange("(m p) -> p m", p=P))
-
-        first_layer(0, 0)
-        round_w1(1, 0)
-        quantize_w1(1, 0)
-        edge_weight = sb("edge_weight", [P, S], F32, tag="picked0")
+        early = [(0, 0), (1, 0), (2, 0), (3, 0), (0, 1)]
+        late = [(1, 1), (2, 1), (3, 1)]
         for half in range(2):
-            cols = slice(HALF * half, HALF * (half + 1))
-            nc.sync.dma_start(out=edge_weight[:, cols], in_=ew[cols].partition_broadcast(P))
-        round_w1(1, 1)
-        quantize_w1(1, 1)
+            gather_words(half, None)
+            part_words(half)
+        for b, (m, half) in enumerate(early):
+            skip_pass(0, m, half, b)
+        for g in range(2):
+            round_w1(0, g)
+            quantize_w1(0, g)
+        first_layer(0, 0)
+        for g in range(2):
+            round_w1(1, g)
+            quantize_w1(1, g)
         first_layer(0, 1)
         quantize_h(0, 0)
         first_layer(1, 0)
         quantize_h(0, 1)
         first_layer(1, 1)
-        for m in range(4):
-            skip_passes(m, 0, 3 + m)
-        skip_passes(0, 1, 7)
-        for m in range(4):
-            second_layer(0, m, 0)
-        second_layer(0, 0, 1)
+        for m, half in early:
+            skip_pass(1, m, half)
+        for m, half in early:
+            second_layer(0, m, half)
         quantize_h(1, 0)
         for m in range(4):
             second_layer(1, m, 0)
-        for m in range(1, 4):
-            skip_passes(m, 1, (m + 1) % 3)
-            second_layer(0, m, 1)
+        for m, half in late:
+            for g in range(2):
+                skip_pass(g, m, half, 5 + m % 3)
+            second_layer(0, m, half)
         quantize_h(1, 1)
-        for m in range(4):
+        biased = sb("biased", [P, 2 * HALF], F32, tag="h_rows11")
+        for m in range(2):
             finish(m, 0)
+            finish_aside(2 + m, 0, biased[:, HALF * m : HALF * (m + 1)])
         for m in range(4):
             second_layer(1, m, 1)
-            finish(m, 1)
+            finish(m, 1, 2 if m == 3 else 1)

@@ -1,6 +1,7 @@
 from contextlib import ExitStack
 
 import concourse.mybir as mybir
+from concourse.masks import make_identity
 
 K, T, S, H, N = 1024, 4096, 1024, 1024, 512
 FLOPS = 2 * S * (K * H + H * N + K * N)
@@ -18,8 +19,8 @@ ACT = mybir.ActivationFunctionType
 
 P = 128
 HALF = 512
-V_SHARE = {(0, 0): 64, (0, 1): 84, (1, 0): 128, (1, 1): 72}
-V_WEAVE_LAST = 344
+QUARTER = 256
+QUARTER_BYTES = 4 * 512 * 4
 
 
 def tile_list_edge_skip_messages_kernel(
@@ -28,6 +29,7 @@ def tile_list_edge_skip_messages_kernel(
     nc = tc.nc
     with ExitStack() as ctx:
         keep = ctx.enter_context(tc.tile_pool(name="keep", bufs=1))
+        land = ctx.enter_context(tc.tile_pool(name="land", bufs=1))
         psum = ctx.enter_context(tc.psum_pool(name="psum", bufs=1))
 
         def sb(name, shape, dtype, tag=None):
@@ -36,13 +38,10 @@ def tile_list_edge_skip_messages_kernel(
         def bank(b, name):
             return psum.tile([P, HALF], F32, name=name, tag="bank%d" % b)
 
-        def w1_rows(a, g):
-            return w1[512 * g : 512 * (g + 1), 512 * a : 512 * (a + 1)].rearrange("(p j) c -> p j c", j=4)
-
-        def load_weight_scales(queue, plane, scales):
+        def load_weight_scales(queues, plane, scales):
             rows = plane[:].bitcast(I32).rearrange("p (a n) -> p a n", a=2)
             for q in range(4):
-                queue.dma_start(
+                queues[q].dma_start(
                     out=rows[32 * q : 32 * q + 4],
                     in_=scales[:, 4 * q : 4 * q + 4, :].rearrange("a r n -> r a n").bitcast(I32),
                 )
@@ -50,124 +49,126 @@ def tile_list_edge_skip_messages_kernel(
         offsets = keep.tile([P, S // 16], U16, name="offsets")
         nc.sync.dma_start(offsets[:], offs)
 
+        ws_plane = sb("ws_plane", [P, 2 * N], U8)
+        v_plane = [sb("v_plane%d" % g, [P, S], U8) for g in range(2)]
+        nc.gpsimd.memset(ws_plane[:].bitcast(I32), 0)
+        ew_cols = sb("ew_cols", [P, 8], F32)
+        nc.scalar.dma_start(out=ew_cols[:], in_=ew.rearrange("(p m) -> p m", m=8))
+        b1_cols = sb("b1_cols", [P, 2, 4], F32)
+        nc.scalar.dma_start(out=b1_cols[:], in_=b1.rearrange("(a p t) -> p a t", a=2, t=4))
+        load_weight_scales([nc.scalar] + [nc.gpsimd] * 3, ws_plane, ws_scales)
+        identity = sb("identity", [P, P], F32)
+        make_identity(nc, identity[:])
+
         word_bytes = 512 * T
-        tab_scales = sb("tab_scales", [P, T], U8)
+        tab_scales = land.tile([P, T], U8, name="tab_scales", offset=QUARTER_BYTES - T // 2)
         nc.sync.dma_start(
             out=tab_scales[:].bitcast(I32)[0:32, :],
             in_=tab[0, word_bytes:].rearrange("(i b) -> i b", i=32).bitcast(I32),
         )
         nc.vector.memset(tab_scales[:].bitcast(I32)[64:P, :], 0)
         nc.vector.memset(tab_scales[:].bitcast(I32)[32:64, :], 0)
-        tab_words = sb("tab_words", [P, T], I32)
+        tab_words = land.tile([P, T], I32, name="tab_words", offset=2 * QUARTER_BYTES)
         nc.sync.dma_start(out=tab_words[:], in_=tab[0, 0:word_bytes].rearrange("(p b) -> p b", p=P).bitcast(I32))
-        ws_plane = sb("ws_plane", [P, 2 * N], U8)
-        nc.gpsimd.memset(ws_plane[:].bitcast(I32), 0)
-        warm = sb("warm", [P, 2], F32)
-        nc.gpsimd.memset(warm[:, 0:1], 0.0)
-        nc.scalar.activation(out=warm[:, 1:2], in_=warm[:, 0:1], func=ACT.Relu)
-        load_weight_scales(nc.gpsimd, ws_plane, ws_scales)
-        b1_cols = sb("b1_cols", [P, 2, 4], F32)
-        nc.gpsimd.dma_start(out=b1_cols[:], in_=b1.rearrange("(a p t) -> p a t", a=2, t=4))
-        v_plane = [sb("v_plane%d" % g, [P, S], U8) for g in range(2)]
-        w2_plane = sb("w2_plane", [P, 2 * N], U8)
-        for plane in (v_plane[0], v_plane[1], w2_plane):
-            nc.vector.memset(plane[:].bitcast(I32), 0)
+        ws_codes = sb("ws_codes", [P, 2 * 4 * N], U8)
+        nc.sync.dma_start(
+            out=ws_codes[:].bitcast(I32).rearrange("p (a n) -> p a n", a=2),
+            in_=ws_words.rearrange("a p n t -> p a (n t)").bitcast(I32),
+        )
 
+        b2_cols = sb("b2_cols", [P, 4], F32)
+        with nc.allow_non_contiguous_dma(reason="one bias value for each partition and row tile"):
+            nc.gpsimd.dma_start(out=b2_cols[:], in_=b2.rearrange("(m p) -> p m", p=P))
+
+        for plane in v_plane:
+            nc.vector.memset(plane[:].bitcast(I32), 0)
         picked_scales = sb("picked_scales", [P, S], U8)
         nc.vector.tensor_copy(picked_scales[:], tab_scales[:].indirect(offsets[:]))
 
-        def place_scale_rows(queue, g):
+        def place_scale_rows(g):
             for q in range(4):
                 first = 16 * g + 4 * q
-                queue.dma_start(
+                nc.sync.dma_start(
                     out=v_plane[g][:].bitcast(I32)[32 * q : 32 * q + 4, :],
                     in_=picked_scales[:].bitcast(I32)[first : first + 4, :],
                 )
 
-        raw, ws_codes = {}, {}
+        raw = {}
 
         def load_w1(a, g):
-            raw[a, g] = sb("raw%d%d" % (a, g), [P, 4, 512], F32)
-            nc.sync.dma_start(out=raw[a, g][:], in_=w1_rows(a, g))
+            raw[a, g] = land.tile([P, 4, 512], F32, name="raw%d%d" % (a, g), offset=QUARTER_BYTES * (2 * a + g))
+            rows = w1[512 * g : 512 * (g + 1), 512 * a : 512 * (a + 1)].rearrange("(p j) c -> p j c", j=4)
+            nc.sync.dma_start(out=raw[a, g][:], in_=rows)
 
-        def load_ws(g):
-            ws_codes[g] = sb("ws_codes%d" % g, [P, 4 * N], U8)
-            nc.sync.dma_start(
-                out=ws_codes[g][:].bitcast(I32), in_=ws_words[g].rearrange("p n t -> p (n t)").bitcast(I32)
-            )
-
-        place_scale_rows(nc.scalar, 0)
-        load_ws(0)
+        place_scale_rows(0)
         load_w1(0, 0)
+        place_scale_rows(1)
         load_w1(0, 1)
-        place_scale_rows(nc.sync, 1)
-        load_w1(1, 0)
-        load_w1(1, 1)
-        load_ws(1)
-        w2_codes = sb("w2_codes", [P, 2 * 2 * N], U8)
-        nc.sync.dma_start(
-            out=w2_codes[:].bitcast(I32).rearrange("p (a n) -> p a n", a=2),
-            in_=w2_words.rearrange("a p n -> p a n").bitcast(I32),
-        )
-        load_weight_scales(nc.sync, w2_plane, w2_scales)
-        b2_cols = sb("b2_cols", [P, 4], F32)
-        with nc.allow_non_contiguous_dma(reason="one bias value for each partition and row tile"):
-            nc.sync.dma_start(out=b2_cols[:], in_=b2.rearrange("(m p) -> p m", p=P))
+
         edge_weight = sb("edge_weight", [P, S], F32)
-        for half in range(2):
-            cols = slice(HALF * half, HALF * (half + 1))
-            nc.sync.dma_start(out=edge_weight[:, cols], in_=ew[cols].partition_broadcast(P))
-
-        picked, v_codes = {}, {}
-
-        def gather_words(half, tag):
-            picked[half] = sb("picked%d" % half, [P, HALF], U32, tag=tag)
-            nc.vector.tensor_copy(
-                picked[half][:], tab_words[:].bitcast(U32).indirect(offsets[:, 32 * half : 32 * (half + 1)])
+        for i in range(2):
+            spread = bank(5 + i, "spread")
+            for m in range(4):
+                column = ew_cols[:, 4 * i + m : 4 * i + m + 1].to_broadcast([P, P])
+                nc.tensor.transpose(spread[:, P * m : P * (m + 1)], column, identity[:])
+            nc.scalar.activation(
+                out=edge_weight[:].rearrange("p (n i m) -> p i n m", i=2, m=4)[:, i],
+                in_=spread[:].rearrange("p (m n) -> p n m", m=4),
+                func=ACT.Copy,
             )
 
-        def part_words(half):
+        v_codes = {}
+
+        def gather_words(half):
+            picked = sb("picked%d" % half, [P, HALF], U32, tag="picked")
+            nc.vector.tensor_copy(
+                picked[:], tab_words[:].bitcast(U32).indirect(offsets[:, 32 * half : 32 * (half + 1)])
+            )
             v_codes[half] = sb("v_codes%d" % half, [P, 4 * HALF], U8)
             nc.vector.tensor_copy(
                 out=v_codes[half][:].bitcast(U16).rearrange("p (g n) -> p g n", g=2),
-                in_=picked[half][:].bitcast(U16).rearrange("p (n g) -> p g n", g=2),
+                in_=picked[:].bitcast(U16).rearrange("p (n g) -> p g n", g=2),
             )
 
         def v_operand(g, half):
             codes = v_codes[half][:, 2 * HALF * g : 2 * HALF * (g + 1)].bitcast(FP4X4)
             return codes, v_plane[g][:, HALF * half : HALF * (half + 1)]
 
-        w1_codes, w1_plane, grouped = {}, {}, {}
+        def copy_on(engine, dst, src):
+            if engine is nc.vector:
+                nc.vector.tensor_copy(out=dst, in_=src)
+            else:
+                nc.scalar.copy(out=dst, in_=src)
 
-        def round_w1(a, g):
-            grouped[a, g] = sb("grouped%d%d" % (a, g), [P, 2048], BF16)
-            dst = grouped[a, g][:].rearrange("p (t m j) -> p m j t", t=4, j=4)
-            src = raw[a, g][:].rearrange("p j (m t) -> p m j t", t=4)
-            share = V_SHARE[a, g]
-            nc.vector.tensor_copy(out=dst[:, 0:share], in_=src[:, 0:share])
-            if share < P:
-                nc.scalar.activation(out=dst[:, share:P], in_=src[:, share:P], func=ACT.Copy)
+        w1_codes, w1_plane = {}, {}
 
-        def quantize_w1(a, g):
-            w1_codes[a, g] = sb("w1_codes%d%d" % (a, g), [P, 512], U32)
-            w1_plane[a, g] = sb("w1_plane%d%d" % (a, g), [P, 512], U8)
-            nc.vector.quantize_mx(out=w1_codes[a, g][:].bitcast(FP8X4), scales=w1_plane[a, g][:], in_=grouped[a, g][:])
+        def quantize_w1(a, g, engines):
+            staged = []
+            for u in range(2):
+                staged.append(sb("grouped%d%d%d" % (a, g, u), [P, 1024], BF16, tag="stage%d" % u))
+                dst = staged[u][:].rearrange("p (t m j) -> p m j t", t=2, j=4)
+                src = raw[a, g][:].rearrange("p j (m t) -> p m j t", t=4)[:, :, :, 2 * u : 2 * u + 2]
+                copy_on(engines[u], dst, src)
+            for u in range(2):
+                w1_codes[a, g, u] = sb("w1_codes%d%d%d" % (a, g, u), [P, 2 * P], U32)
+                w1_plane[a, g, u] = sb("w1_plane%d%d%d" % (a, g, u), [P, 2 * P], U8)
+                nc.vector.quantize_mx(
+                    out=w1_codes[a, g, u][:].bitcast(FP8X4), scales=w1_plane[a, g, u][:], in_=staged[u][:]
+                )
 
         h_rows, h_codes, h_plane = {}, {}, {}
 
         def first_layer(a, half):
-            h_rows[a, half] = sb(
-                "h_rows%d%d" % (a, half), [P, 4, HALF], BF16, tag="raw11" if (a, half) == (0, 1) else None
-            )
+            h_rows[a, half] = sb("h_rows%d%d" % (a, half), [P, 4, HALF], BF16)
             for t in range(4):
                 acc = bank(5 + (8 * a + 4 * half + t) % 3, "h_acc")
-                cols = slice(P * t, P * (t + 1))
+                cols = slice(P * (t % 2), P * (t % 2 + 1))
                 for g in range(2):
                     codes, plane = v_operand(g, half)
                     nc.tensor.matmul_mx(
                         out=acc[:],
-                        lhsT=w1_codes[a, g][:, cols].bitcast(FP8X4),
-                        lhsT_scale=w1_plane[a, g][:, cols],
+                        lhsT=w1_codes[a, g, t // 2][:, cols].bitcast(FP8X4),
+                        lhsT_scale=w1_plane[a, g, t // 2][:, cols],
                         rhs=codes,
                         rhs_scale=plane,
                         start=(g == 0),
@@ -177,33 +178,38 @@ def tile_list_edge_skip_messages_kernel(
                     out=h_rows[a, half][:, t, :], in_=acc[:], func=ACT.Relu, bias=b1_cols[:, a, t : t + 1]
                 )
 
-        def quantize_h(a, half):
-            woven = sb("h_woven%d%d" % (a, half), [P, 4 * HALF], BF16, tag="grouped11" if (a, half) == (0, 0) else None)
-            dst = woven[:].rearrange("p (c i t) -> p c t i", i=4, t=4)
-            src = h_rows[a, half][:].rearrange("p t (c i) -> p c t i", i=4)
-            share = V_WEAVE_LAST // 4 if (a, half) == (1, 1) else P
-            nc.vector.tensor_copy(out=dst[:, 0:share], in_=src[:, 0:share])
-            if share < P:
-                nc.scalar.copy(out=dst[:, share:P], in_=src[:, share:P])
+        def quantize_h(a, half, engines):
             h_codes[a, half] = sb("h_codes%d%d" % (a, half), [P, HALF], U32)
             h_plane[a, half] = sb("h_plane%d%d" % (a, half), [P, HALF], U8)
-            nc.vector.quantize_mx(out=h_codes[a, half][:].bitcast(FP8X4), scales=h_plane[a, half][:], in_=woven[:])
+            woven = []
+            for u in range(2):
+                tag = "stage%d" % u if a == 0 else None
+                woven.append(sb("h_woven%d%d%d" % (a, half, u), [P, 4 * QUARTER], BF16, tag=tag))
+                dst = woven[u][:].rearrange("p (c i t) -> p c t i", i=4, t=4)
+                src = h_rows[a, half][:, :, QUARTER * u : QUARTER * (u + 1)].rearrange("p t (c i) -> p c t i", i=4)
+                copy_on(engines[u], dst, src)
+            for u in range(2):
+                cols = slice(QUARTER * u, QUARTER * (u + 1))
+                nc.vector.quantize_mx(
+                    out=h_codes[a, half][:, cols].bitcast(FP8X4), scales=h_plane[a, half][:, cols], in_=woven[u][:]
+                )
 
         y_acc = {}
 
-        def skip_pass(g, m, half, b=None):
-            if g == 0:
-                y_acc[m, half] = bank(b, "y_acc")
-            codes, plane = v_operand(g, half)
-            nc.tensor.matmul_mx(
-                out=y_acc[m, half][:],
-                lhsT=ws_codes[g][:, 4 * P * m : 4 * P * (m + 1)].bitcast(FP8X4),
-                lhsT_scale=ws_plane[:, N * g + P * m : N * g + P * (m + 1)],
-                rhs=codes,
-                rhs_scale=plane,
-                start=(g == 0),
-                stop=False,
-            )
+        def skip_passes(m, half, b):
+            y_acc[m, half] = bank(b, "y_acc")
+            for g in range(2):
+                codes, plane = v_operand(g, half)
+                first = N * g + P * m
+                nc.tensor.matmul_mx(
+                    out=y_acc[m, half][:],
+                    lhsT=ws_codes[:, 4 * first : 4 * (first + P)].bitcast(FP8X4),
+                    lhsT_scale=ws_plane[:, first : first + P],
+                    rhs=codes,
+                    rhs_scale=plane,
+                    start=(g == 0),
+                    stop=False,
+                )
 
         def second_layer(a, m, half):
             first = N * a + P * m
@@ -217,63 +223,58 @@ def tile_list_edge_skip_messages_kernel(
                 stop=(a == 1),
             )
 
-        def finish(m, half, pieces=1):
-            width = HALF // pieces
-            for i in range(pieces):
-                result = sb("result%d%d%d" % (m, half, i), [P, width], F32)
-                cols = slice(HALF * half + width * i, HALF * half + width * (i + 1))
-                nc.vector.scalar_tensor_tensor(
-                    out=result[:],
-                    in0=y_acc[m, half][:, width * i : width * (i + 1)],
-                    scalar=b2_cols[:, m : m + 1],
-                    in1=edge_weight[:, cols],
-                    op0=ALU.add,
-                    op1=ALU.mult,
-                )
-                nc.sync.dma_start(out=out[P * m : P * (m + 1), cols], in_=result[:])
-
-        def finish_aside(m, half, biased):
+        def finish(m, half):
             result = sb("result%d%d" % (m, half), [P, HALF], F32)
             cols = slice(HALF * half, HALF * (half + 1))
-            nc.scalar.activation(out=biased, in_=y_acc[m, half][:], func=ACT.Identity, bias=b2_cols[:, m : m + 1])
-            nc.gpsimd.tensor_tensor(out=result[:], in0=biased, in1=edge_weight[:, cols], op=ALU.mult)
+            nc.vector.scalar_tensor_tensor(
+                out=result[:],
+                in0=y_acc[m, half][:],
+                scalar=b2_cols[:, m : m + 1],
+                in1=edge_weight[:, cols],
+                op0=ALU.add,
+                op1=ALU.mult,
+            )
             nc.sync.dma_start(out=out[P * m : P * (m + 1), cols], in_=result[:])
 
+        both = (nc.vector, nc.scalar)
+        alone = (nc.vector, nc.vector)
         early = [(0, 0), (1, 0), (2, 0), (3, 0), (0, 1)]
         late = [(1, 1), (2, 1), (3, 1)]
         for half in range(2):
-            gather_words(half, None)
-            part_words(half)
+            gather_words(half)
+        load_w1(1, 0)
+        load_w1(1, 1)
+        w2_codes = sb("w2_codes", [P, 2 * 2 * N], U8, tag="picked")
+        nc.sync.dma_start(
+            out=w2_codes[:].bitcast(I32).rearrange("p (a n) -> p a n", a=2),
+            in_=w2_words.rearrange("a p n -> p a n").bitcast(I32),
+        )
+        w2_plane = sb("w2_plane", [P, 2 * N], U8, tag="picked_scales")
+        nc.gpsimd.memset(w2_plane[:].bitcast(I32), 0)
+        load_weight_scales([nc.sync] * 4, w2_plane, w2_scales)
+        for g in range(2):
+            quantize_w1(0, g, both)
+        for half in range(2):
+            first_layer(0, half)
+        for g in range(2):
+            quantize_w1(1, g, alone)
+        for half in range(2):
+            first_layer(1, half)
         for b, (m, half) in enumerate(early):
-            skip_pass(0, m, half, b)
-        for g in range(2):
-            round_w1(0, g)
-            quantize_w1(0, g)
-        first_layer(0, 0)
-        for g in range(2):
-            round_w1(1, g)
-            quantize_w1(1, g)
-        first_layer(0, 1)
-        quantize_h(0, 0)
-        first_layer(1, 0)
-        quantize_h(0, 1)
-        first_layer(1, 1)
-        for m, half in early:
-            skip_pass(1, m, half)
+            skip_passes(m, half, b)
+        for half in range(2):
+            quantize_h(0, half, alone)
+        for half in range(2):
+            quantize_h(1, half, both)
         for m, half in early:
             second_layer(0, m, half)
-        quantize_h(1, 0)
         for m in range(4):
             second_layer(1, m, 0)
-        for m, half in late:
-            for g in range(2):
-                skip_pass(g, m, half, 5 + m % 3)
-            second_layer(0, m, half)
-        quantize_h(1, 1)
-        biased = sb("biased", [P, 2 * HALF], F32, tag="h_rows11")
-        for m in range(2):
-            finish(m, 0)
-            finish_aside(2 + m, 0, biased[:, HALF * m : HALF * (m + 1)])
         for m in range(4):
+            finish(m, 0)
+        for m in range(4):
+            if (m, 1) in late:
+                skip_passes(m, 1, 4 + m)
+                second_layer(0, m, 1)
             second_layer(1, m, 1)
-            finish(m, 1, 2 if m == 3 else 1)
+            finish(m, 1)

@@ -76,9 +76,6 @@ def tile_list_edge_skip_messages_kernel(
             in_=ws_words.rearrange("a p n t -> p a (n t)").bitcast(I32),
         )
 
-        b2_cols = sb("b2_cols", [P, 4], F32)
-        with nc.allow_non_contiguous_dma(reason="one bias value for each partition and row tile"):
-            nc.gpsimd.dma_start(out=b2_cols[:], in_=b2.rearrange("(m p) -> p m", p=P))
 
         for plane in v_plane:
             nc.vector.memset(plane[:].bitcast(I32), 0)
@@ -107,7 +104,7 @@ def tile_list_edge_skip_messages_kernel(
 
         edge_weight = sb("edge_weight", [P, S], F32)
         for i in range(2):
-            spread = bank(5 + i, "spread")
+            spread = bank(4 + i, "spread")
             for m in range(4):
                 column = ew_cols[:, 4 * i + m : 4 * i + m + 1].to_broadcast([P, P])
                 nc.tensor.transpose(spread[:, P * m : P * (m + 1)], column, identity[:])
@@ -161,7 +158,7 @@ def tile_list_edge_skip_messages_kernel(
         def first_layer(a, half):
             h_rows[a, half] = sb("h_rows%d%d" % (a, half), [P, 4, HALF], BF16)
             for t in range(4):
-                acc = bank(5 + (8 * a + 4 * half + t) % 3, "h_acc")
+                acc = bank(4 + t, "h_acc")
                 cols = slice(P * (t % 2), P * (t % 2 + 1))
                 for g in range(2):
                     codes, plane = v_operand(g, half)
@@ -223,23 +220,23 @@ def tile_list_edge_skip_messages_kernel(
                 stop=(a == 1),
             )
 
-        def finish(m, half):
-            result = sb("result%d%d" % (m, half), [P, HALF], F32)
-            cols = slice(HALF * half, HALF * (half + 1))
-            nc.vector.scalar_tensor_tensor(
-                out=result[:],
-                in0=y_acc[m, half][:],
-                scalar=b2_cols[:, m : m + 1],
-                in1=edge_weight[:, cols],
-                op0=ALU.add,
-                op1=ALU.mult,
-            )
-            nc.sync.dma_start(out=out[P * m : P * (m + 1), cols], in_=result[:])
+        def finish(m, half, pieces=1):
+            width = HALF // pieces
+            for i in range(pieces):
+                result = sb("result%d%d%d" % (m, half, i), [P, width], F32)
+                cols = slice(HALF * half + width * i, HALF * half + width * (i + 1))
+                nc.vector.scalar_tensor_tensor(
+                    out=result[:],
+                    in0=y_acc[m, half][:, width * i : width * (i + 1)],
+                    scalar=b2_cols[:, m : m + 1],
+                    in1=edge_weight[:, cols],
+                    op0=ALU.add,
+                    op1=ALU.mult,
+                )
+                nc.sync.dma_start(out=out[P * m : P * (m + 1), cols], in_=result[:])
 
         both = (nc.vector, nc.scalar)
         alone = (nc.vector, nc.vector)
-        early = [(0, 0), (1, 0), (2, 0), (3, 0), (0, 1)]
-        late = [(1, 1), (2, 1), (3, 1)]
         for half in range(2):
             gather_words(half)
         load_w1(1, 0)
@@ -252,6 +249,9 @@ def tile_list_edge_skip_messages_kernel(
         w2_plane = sb("w2_plane", [P, 2 * N], U8, tag="picked_scales")
         nc.gpsimd.memset(w2_plane[:].bitcast(I32), 0)
         load_weight_scales([nc.sync] * 4, w2_plane, w2_scales)
+        b2_cols = land.tile([P, 4], F32, name="b2_cols", offset=0)
+        with nc.allow_non_contiguous_dma(reason="one bias value for each partition and row tile"):
+            nc.sync.dma_start(out=b2_cols[:], in_=b2.rearrange("(m p) -> p m", p=P))
         for g in range(2):
             quantize_w1(0, g, both)
         for half in range(2):
@@ -260,21 +260,19 @@ def tile_list_edge_skip_messages_kernel(
             quantize_w1(1, g, alone)
         for half in range(2):
             first_layer(1, half)
-        for b, (m, half) in enumerate(early):
-            skip_passes(m, half, b)
+        for m in range(4):
+            skip_passes(m, 0, m)
         for half in range(2):
             quantize_h(0, half, alone)
-        for half in range(2):
-            quantize_h(1, half, both)
-        for m, half in early:
-            second_layer(0, m, half)
-        for m in range(4):
-            second_layer(1, m, 0)
+        quantize_h(1, 0, alone)
+        quantize_h(1, 1, both)
+        for a in range(2):
+            for m in range(4):
+                second_layer(a, m, 0)
         for m in range(4):
             finish(m, 0)
         for m in range(4):
-            if (m, 1) in late:
-                skip_passes(m, 1, 4 + m)
-                second_layer(0, m, 1)
-            second_layer(1, m, 1)
-            finish(m, 1)
+            skip_passes(m, 1, 4 + m)
+            for a in range(2):
+                second_layer(a, m, 1)
+            finish(m, 1, 2 if m == 3 else 1)

@@ -20,7 +20,21 @@ ACT = mybir.ActivationFunctionType
 P = 128
 HALF = 512
 QUARTER = 256
-QUARTER_BYTES = 4 * 512 * 4
+LAP = 64
+RAW = 4 * 512 * 4
+STAGE = 2 * 1024
+AT_RAW00 = 0
+AT_RAW01 = RAW
+AT_SCALES = 2 * RAW - LAP
+AT_WS = AT_SCALES + T
+AT_PICKED = (AT_WS + 4096 - LAP, AT_WS + 4096 - LAP + 2048)
+AT_W2 = AT_PICKED[0] + LAP
+AT_FIRST_CODES = (AT_PICKED[1] + LAP, AT_PICKED[1] + LAP + 1024)
+AT_STAGE = [AT_FIRST_CODES[1] + 1024 + STAGE * i for i in range(4)]
+AT_LATE_PLANE = AT_STAGE[3] - 256
+AT_WORDS = AT_STAGE[3] + STAGE
+AT_RAW10 = AT_WORDS
+AT_RAW11 = AT_WORDS + RAW
 
 
 def tile_list_edge_skip_messages_kernel(
@@ -35,13 +49,16 @@ def tile_list_edge_skip_messages_kernel(
         def sb(name, shape, dtype, tag=None):
             return keep.tile(shape, dtype, name=name, tag=tag or name, align_bytes=64)
 
+        def at(offset, name, shape, dtype):
+            return land.tile(shape, dtype, name=name, offset=offset, align_bytes=64)
+
         def bank(b, name):
             return psum.tile([P, HALF], F32, name=name, tag="bank%d" % b)
 
-        def load_weight_scales(queues, plane, scales):
-            rows = plane[:].bitcast(I32).rearrange("p (a n) -> p a n", a=2)
+        def load_weight_scales(plane, scales):
+            rows = plane.bitcast(I32).rearrange("p (a n) -> p a n", a=2)
             for q in range(4):
-                queues[q].dma_start(
+                nc.sync.dma_start(
                     out=rows[32 * q : 32 * q + 4],
                     in_=scales[:, 4 * q : 4 * q + 4, :].rearrange("a r n -> r a n").bitcast(I32),
                 )
@@ -49,33 +66,32 @@ def tile_list_edge_skip_messages_kernel(
         offsets = keep.tile([P, S // 16], U16, name="offsets")
         nc.sync.dma_start(offsets[:], offs)
 
-        ws_plane = sb("ws_plane", [P, 2 * N], U8)
-        v_plane = [sb("v_plane%d" % g, [P, S], U8) for g in range(2)]
-        nc.gpsimd.memset(ws_plane[:].bitcast(I32), 0)
         ew_cols = sb("ew_cols", [P, 8], F32)
         nc.scalar.dma_start(out=ew_cols[:], in_=ew.rearrange("(p m) -> p m", m=8))
-        b1_cols = sb("b1_cols", [P, 2, 4], F32)
-        nc.scalar.dma_start(out=b1_cols[:], in_=b1.rearrange("(a p t) -> p a t", a=2, t=4))
-        load_weight_scales([nc.scalar] + [nc.gpsimd] * 3, ws_plane, ws_scales)
         identity = sb("identity", [P, P], F32)
         make_identity(nc, identity[:])
+        b1_cols = sb("b1_cols", [P, 2, 4], F32)
+        nc.gpsimd.dma_start(out=b1_cols[:], in_=b1.rearrange("(a p t) -> p a t", a=2, t=4))
+        v_plane = [sb("v_plane%d" % g, [P, S], U8) for g in range(2)]
+
+        raw = {}
+
+        def load_w1(a, g, offset):
+            raw[a, g] = at(offset, "raw%d%d" % (a, g), [P, 4, 512], F32)
+            rows = w1[512 * g : 512 * (g + 1), 512 * a : 512 * (a + 1)].rearrange("(p j) c -> p j c", j=4)
+            nc.sync.dma_start(out=raw[a, g][:], in_=rows)
 
         word_bytes = 512 * T
-        tab_scales = land.tile([P, T], U8, name="tab_scales", offset=QUARTER_BYTES - T // 2)
+        tab_scales = at(AT_SCALES, "tab_scales", [P, T], U8)
         nc.sync.dma_start(
             out=tab_scales[:].bitcast(I32)[0:32, :],
             in_=tab[0, word_bytes:].rearrange("(i b) -> i b", i=32).bitcast(I32),
         )
         nc.vector.memset(tab_scales[:].bitcast(I32)[64:P, :], 0)
         nc.vector.memset(tab_scales[:].bitcast(I32)[32:64, :], 0)
-        tab_words = land.tile([P, T], I32, name="tab_words", offset=2 * QUARTER_BYTES)
+        tab_words = at(AT_WORDS, "tab_words", [P, T], I32)
         nc.sync.dma_start(out=tab_words[:], in_=tab[0, 0:word_bytes].rearrange("(p b) -> p b", p=P).bitcast(I32))
-        ws_codes = sb("ws_codes", [P, 2 * 4 * N], U8)
-        nc.sync.dma_start(
-            out=ws_codes[:].bitcast(I32).rearrange("p (a n) -> p a n", a=2),
-            in_=ws_words.rearrange("a p n t -> p a (n t)").bitcast(I32),
-        )
-
+        load_w1(0, 0, AT_RAW00)
 
         for plane in v_plane:
             nc.vector.memset(plane[:].bitcast(I32), 0)
@@ -90,17 +106,12 @@ def tile_list_edge_skip_messages_kernel(
                     in_=picked_scales[:].bitcast(I32)[first : first + 4, :],
                 )
 
-        raw = {}
-
-        def load_w1(a, g):
-            raw[a, g] = land.tile([P, 4, 512], F32, name="raw%d%d" % (a, g), offset=QUARTER_BYTES * (2 * a + g))
-            rows = w1[512 * g : 512 * (g + 1), 512 * a : 512 * (a + 1)].rearrange("(p j) c -> p j c", j=4)
-            nc.sync.dma_start(out=raw[a, g][:], in_=rows)
-
         place_scale_rows(0)
-        load_w1(0, 0)
+        load_w1(0, 1, AT_RAW01)
         place_scale_rows(1)
-        load_w1(0, 1)
+        weight_planes = at(AT_SCALES + LAP, "weight_planes", [P, 2, 2 * N], U8)
+        nc.vector.memset(weight_planes[:].rearrange("p w n -> p (w n)").bitcast(I32), 0)
+        ws_plane, w2_plane = weight_planes[:, 0], weight_planes[:, 1]
 
         edge_weight = sb("edge_weight", [P, S], F32)
         for i in range(2):
@@ -117,7 +128,7 @@ def tile_list_edge_skip_messages_kernel(
         v_codes = {}
 
         def gather_words(half):
-            picked = sb("picked%d" % half, [P, HALF], U32, tag="picked")
+            picked = at(AT_PICKED[half], "picked%d" % half, [P, HALF], U32)
             nc.vector.tensor_copy(
                 picked[:], tab_words[:].bitcast(U32).indirect(offsets[:, 32 * half : 32 * (half + 1)])
             )
@@ -139,85 +150,94 @@ def tile_list_edge_skip_messages_kernel(
 
         w1_codes, w1_plane = {}, {}
 
-        def quantize_w1(a, g, engines):
-            staged = []
-            for u in range(2):
-                staged.append(sb("grouped%d%d%d" % (a, g, u), [P, 1024], BF16, tag="stage%d" % u))
-                dst = staged[u][:].rearrange("p (t m j) -> p m j t", t=2, j=4)
-                src = raw[a, g][:].rearrange("p j (m t) -> p m j t", t=4)[:, :, :, 2 * u : 2 * u + 2]
-                copy_on(engines[u], dst, src)
-            for u in range(2):
-                w1_codes[a, g, u] = sb("w1_codes%d%d%d" % (a, g, u), [P, 2 * P], U32)
-                w1_plane[a, g, u] = sb("w1_plane%d%d%d" % (a, g, u), [P, 2 * P], U8)
-                nc.vector.quantize_mx(
-                    out=w1_codes[a, g, u][:].bitcast(FP8X4), scales=w1_plane[a, g, u][:], in_=staged[u][:]
-                )
+        staged = {}
 
-        h_rows, h_codes, h_plane = {}, {}, {}
+        def round_w1(a, g, u, engine, slot):
+            staged[a, g, u] = at(AT_STAGE[slot], "grouped%d%d%d" % (a, g, u), [P, 1024], BF16)
+            dst = staged[a, g, u][:].rearrange("p (t m j) -> p m j t", t=2, j=4)
+            src = raw[a, g][:].rearrange("p j (m t) -> p m j t", t=4)[:, :, :, 2 * u : 2 * u + 2]
+            copy_on(engine, dst, src)
 
-        def first_layer(a, half):
-            h_rows[a, half] = sb("h_rows%d%d" % (a, half), [P, 4, HALF], BF16)
-            for t in range(4):
-                acc = bank(4 + t, "h_acc")
-                cols = slice(P * (t % 2), P * (t % 2 + 1))
-                for g in range(2):
-                    codes, plane = v_operand(g, half)
-                    nc.tensor.matmul_mx(
-                        out=acc[:],
-                        lhsT=w1_codes[a, g, t // 2][:, cols].bitcast(FP8X4),
-                        lhsT_scale=w1_plane[a, g, t // 2][:, cols],
-                        rhs=codes,
-                        rhs_scale=plane,
-                        start=(g == 0),
-                        stop=(g == 1),
-                    )
+        def quantize_w1(a, g, u):
+            name = "w1_codes%d%d%d" % (a, g, u)
+            if (a, g) == (0, 0):
+                w1_codes[a, g, u] = at(AT_FIRST_CODES[u], name, [P, 2 * P], U32)
+            else:
+                w1_codes[a, g, u] = sb(name, [P, 2 * P], U32)
+            w1_plane[a, g, u] = sb("w1_plane%d%d%d" % (a, g, u), [P, 2 * P], U8)
+            nc.vector.quantize_mx(
+                out=w1_codes[a, g, u][:].bitcast(FP8X4), scales=w1_plane[a, g, u][:], in_=staged[a, g, u][:]
+            )
+
+        h_rows, h_codes, h_plane, h_acc = {}, {}, {}, {}
+
+        def first_layer(a, half, t, g, last):
+            if not last:
+                h_acc[half, t] = bank(4 * half + t, "h_acc")
+            cols = slice(P * (t % 2), P * (t % 2 + 1))
+            codes, plane = v_operand(g, half)
+            nc.tensor.matmul_mx(
+                out=h_acc[half, t][:],
+                lhsT=w1_codes[a, g, t // 2][:, cols].bitcast(FP8X4),
+                lhsT_scale=w1_plane[a, g, t // 2][:, cols],
+                rhs=codes,
+                rhs_scale=plane,
+                start=not last,
+                stop=last,
+            )
+            if last:
+                if t == 0:
+                    h_rows[a, half] = sb("h_rows%d%d" % (a, half), [P, 4, HALF], BF16)
                 nc.scalar.activation(
-                    out=h_rows[a, half][:, t, :], in_=acc[:], func=ACT.Relu, bias=b1_cols[:, a, t : t + 1]
+                    out=h_rows[a, half][:, t, :], in_=h_acc[half, t][:], func=ACT.Relu, bias=b1_cols[:, a, t : t + 1]
                 )
 
-        def quantize_h(a, half, engines):
-            h_codes[a, half] = sb("h_codes%d%d" % (a, half), [P, HALF], U32)
-            h_plane[a, half] = sb("h_plane%d%d" % (a, half), [P, HALF], U8)
-            woven = []
-            for u in range(2):
-                tag = "stage%d" % u if a == 0 else None
-                woven.append(sb("h_woven%d%d%d" % (a, half, u), [P, 4 * QUARTER], BF16, tag=tag))
-                dst = woven[u][:].rearrange("p (c i t) -> p c t i", i=4, t=4)
-                src = h_rows[a, half][:, :, QUARTER * u : QUARTER * (u + 1)].rearrange("p t (c i) -> p c t i", i=4)
-                copy_on(engines[u], dst, src)
-            for u in range(2):
-                cols = slice(QUARTER * u, QUARTER * (u + 1))
-                nc.vector.quantize_mx(
-                    out=h_codes[a, half][:, cols].bitcast(FP8X4), scales=h_plane[a, half][:, cols], in_=woven[u][:]
-                )
+        woven = {}
+
+        def weave_h(a, half, u, engine, slot=None):
+            name = "h_woven%d%d%d" % (a, half, u)
+            if engine is nc.vector:
+                woven[a, half, u] = at(AT_STAGE[slot], name, [P, 4 * QUARTER], BF16)
+            else:
+                woven[a, half, u] = sb(name, [P, 4 * QUARTER], BF16)
+            dst = woven[a, half, u][:].rearrange("p (c i t) -> p c t i", i=4, t=4)
+            src = h_rows[a, half][:, :, QUARTER * u : QUARTER * (u + 1)].rearrange("p t (c i) -> p c t i", i=4)
+            copy_on(engine, dst, src)
+
+        def quantize_h(a, half, u):
+            if (a, half) not in h_codes:
+                h_codes[a, half] = sb("h_codes%d%d" % (a, half), [P, HALF], U32)
+                if (a, half) == (0, 1):
+                    h_plane[a, half] = at(AT_LATE_PLANE, "h_plane01", [P, HALF], U8)
+                else:
+                    h_plane[a, half] = sb("h_plane%d%d" % (a, half), [P, HALF], U8)
+            cols = slice(QUARTER * u, QUARTER * (u + 1))
+            nc.vector.quantize_mx(
+                out=h_codes[a, half][:, cols].bitcast(FP8X4), scales=h_plane[a, half][:, cols], in_=woven[a, half, u][:]
+            )
 
         y_acc = {}
 
-        def skip_passes(m, half, b):
-            y_acc[m, half] = bank(b, "y_acc")
-            for g in range(2):
-                codes, plane = v_operand(g, half)
-                first = N * g + P * m
-                nc.tensor.matmul_mx(
-                    out=y_acc[m, half][:],
-                    lhsT=ws_codes[:, 4 * first : 4 * (first + P)].bitcast(FP8X4),
-                    lhsT_scale=ws_plane[:, first : first + P],
-                    rhs=codes,
-                    rhs_scale=plane,
-                    start=(g == 0),
-                    stop=False,
-                )
-
-        def second_layer(a, m, half):
-            first = N * a + P * m
+        def output_pass(kind, i, m, half, start=False, stop=False):
+            if start:
+                y_acc[m, half] = bank(4 * half + m, "y_acc")
+            first = N * i + P * m
+            if kind == "skip":
+                weights = ws_codes[:, 4 * first : 4 * (first + P)].bitcast(FP8X4)
+                weight_plane = ws_plane[:, first : first + P]
+                codes, plane = v_operand(i, half)
+            else:
+                weights = w2_codes[:, 2 * first : 2 * (first + P)].bitcast(FP4X4)
+                weight_plane = w2_plane[:, first : first + P]
+                codes, plane = h_codes[i, half][:].bitcast(FP8X4), h_plane[i, half][:]
             nc.tensor.matmul_mx(
                 out=y_acc[m, half][:],
-                lhsT=w2_codes[:, 2 * first : 2 * (first + P)].bitcast(FP4X4),
-                lhsT_scale=w2_plane[:, first : first + P],
-                rhs=h_codes[a, half][:].bitcast(FP8X4),
-                rhs_scale=h_plane[a, half][:],
-                start=False,
-                stop=(a == 1),
+                lhsT=weights,
+                lhsT_scale=weight_plane,
+                rhs=codes,
+                rhs_scale=plane,
+                start=start,
+                stop=stop,
             )
 
         def finish(m, half, pieces=1):
@@ -235,44 +255,82 @@ def tile_list_edge_skip_messages_kernel(
                 )
                 nc.sync.dma_start(out=out[P * m : P * (m + 1), cols], in_=result[:])
 
-        both = (nc.vector, nc.scalar)
-        alone = (nc.vector, nc.vector)
         for half in range(2):
             gather_words(half)
-        load_w1(1, 0)
-        load_w1(1, 1)
-        w2_codes = sb("w2_codes", [P, 2 * 2 * N], U8, tag="picked")
+        load_w1(1, 0, AT_RAW10)
+        load_w1(1, 1, AT_RAW11)
+        ws_codes = at(AT_WS, "ws_codes", [P, 2 * 4 * N], U8)
+        nc.sync.dma_start(
+            out=ws_codes[:].bitcast(I32).rearrange("p (a n) -> p a n", a=2),
+            in_=ws_words.rearrange("a p n t -> p a (n t)").bitcast(I32),
+        )
+        load_weight_scales(ws_plane, ws_scales)
+        w2_codes = at(AT_W2, "w2_codes", [P, 2 * 2 * N], U8)
         nc.sync.dma_start(
             out=w2_codes[:].bitcast(I32).rearrange("p (a n) -> p a n", a=2),
             in_=w2_words.rearrange("a p n -> p a n").bitcast(I32),
         )
-        w2_plane = sb("w2_plane", [P, 2 * N], U8, tag="picked_scales")
-        nc.gpsimd.memset(w2_plane[:].bitcast(I32), 0)
-        load_weight_scales([nc.sync] * 4, w2_plane, w2_scales)
-        b2_cols = land.tile([P, 4], F32, name="b2_cols", offset=0)
+        load_weight_scales(w2_plane, w2_scales)
+
+        for u in range(2):
+            round_w1(0, 0, u, nc.scalar, u)
+            quantize_w1(0, 0, u)
+        b2_cols = at(AT_RAW00, "b2_cols", [P, 4], F32)
         with nc.allow_non_contiguous_dma(reason="one bias value for each partition and row tile"):
             nc.sync.dma_start(out=b2_cols[:], in_=b2.rearrange("(m p) -> p m", p=P))
-        for g in range(2):
-            quantize_w1(0, g, both)
+        for t in range(4):
+            for half in range(2):
+                first_layer(0, half, t, 0, False)
+        round_w1(0, 1, 0, nc.scalar, 2)
+        round_w1(0, 1, 1, nc.vector, 1)
+        for u in range(2):
+            quantize_w1(0, 1, u)
         for half in range(2):
-            first_layer(0, half)
+            for t in range(4):
+                first_layer(0, half, t, 1, True)
         for g in range(2):
-            quantize_w1(1, g, alone)
-        for half in range(2):
-            first_layer(1, half)
+            for u in range(2):
+                round_w1(1, g, u, nc.vector, u)
+            for u in range(2):
+                quantize_w1(1, g, u)
+        for g in range(2):
+            for t in range(4):
+                first_layer(1, 0, t, g, g == 1)
+        for t in range(4):
+            order = (0, 1) if t < 2 else (1, 0)
+            for g in order:
+                first_layer(1, 1, t, g, g == order[1])
+        for u in range(2):
+            weave_h(0, 0, u, nc.vector, u)
+        for u in range(2):
+            quantize_h(0, 0, u)
+        for u in range(2):
+            weave_h(0, 1, u, nc.vector, u)
+        for u in range(2):
+            weave_h(1, 0, u, nc.vector, 2 + u)
+        for a, half in ((1, 0), (0, 1)):
+            for u in range(2):
+                quantize_h(a, half, u)
+        for u in range(2):
+            weave_h(1, 1, u, nc.scalar)
+            quantize_h(1, 1, u)
         for m in range(4):
-            skip_passes(m, 0, m)
-        for half in range(2):
-            quantize_h(0, half, alone)
-        quantize_h(1, 0, alone)
-        quantize_h(1, 1, both)
+            for g in range(2):
+                output_pass("skip", g, m, 0, start=g == 0)
         for a in range(2):
             for m in range(4):
-                second_layer(a, m, 0)
+                output_pass("layer", a, m, 0, stop=a == 1)
         for m in range(4):
             finish(m, 0)
-        for m in range(4):
-            skip_passes(m, 1, 4 + m)
-            for a in range(2):
-                second_layer(a, m, 1)
-            finish(m, 1, 2 if m == 3 else 1)
+        for pair in range(2):
+            for m in (2 * pair, 2 * pair + 1):
+                output_pass("layer", 0, m, 1, start=True)
+                for g in range(2):
+                    output_pass("skip", g, m, 1)
+                if pair == 1:
+                    output_pass("layer", 1, m, 1, stop=True)
+                    finish(m, 1, 2 if m == 3 else 1)
+            if pair == 0:
+                for m in range(2):
+                    output_pass("layer", 1, m, 1, stop=True)
+                    finish(m, 1)

@@ -68,6 +68,8 @@ def tile_list_edge_skip_messages_kernel(
 
         ew_cols = sb("ew_cols", [P, 8], F32)
         nc.scalar.dma_start(out=ew_cols[:], in_=ew.rearrange("(p m) -> p m", m=8))
+        ones = sb("ones", [P, 4 * P], BF16)
+        nc.gpsimd.memset(ones[:], 1.0)
         identity = sb("identity", [P, P], F32)
         make_identity(nc, identity[:])
         b1_cols = sb("b1_cols", [P, 2, 4], F32)
@@ -125,6 +127,21 @@ def tile_list_edge_skip_messages_kernel(
                 func=ACT.Copy,
             )
 
+        warm_codes = sb("warm_codes", [P, P], U32)
+        warm_plane = sb("warm_plane", [P, P], U8)
+        nc.vector.quantize_mx(out=warm_codes[:].bitcast(FP8X4), scales=warm_plane[:], in_=ones[:])
+
+        def warm_up(acc, codes, plane, start, stop):
+            nc.tensor.matmul_mx(
+                out=acc[:],
+                lhsT=warm_codes[:].bitcast(FP8X4),
+                lhsT_scale=warm_plane[:],
+                rhs=codes,
+                rhs_scale=plane,
+                start=start,
+                stop=stop,
+            )
+
         v_codes = {}
 
         def gather_words(half):
@@ -132,6 +149,10 @@ def tile_list_edge_skip_messages_kernel(
             nc.vector.tensor_copy(
                 picked[:], tab_words[:].bitcast(U32).indirect(offsets[:, 32 * half : 32 * (half + 1)])
             )
+            if half == 0:
+                unread = bank(5, "unread")
+                for i in range(4):
+                    warm_up(unread, picked[:, 0:QUARTER].bitcast(FP4X4), picked_scales[:, 0:HALF], i == 0, i == 3)
             v_codes[half] = sb("v_codes%d" % half, [P, 4 * HALF], U8)
             nc.vector.tensor_copy(
                 out=v_codes[half][:].bitcast(U16).rearrange("p (g n) -> p g n", g=2),

@@ -20,6 +20,7 @@ ACT = mybir.ActivationFunctionType
 P = 128
 HALF = 512
 QUARTER = 256
+VECTOR_SHARE = 84
 LAP = 64
 RAW = 4 * 512 * 4
 STAGE = 2 * 1024
@@ -27,14 +28,16 @@ AT_RAW00 = 0
 AT_RAW01 = RAW
 AT_SCALES = 2 * RAW - LAP
 AT_WS = AT_SCALES + T
-AT_PICKED = (AT_WS + 4096 - LAP, AT_WS + 4096 - LAP + 2048)
-AT_W2 = AT_PICKED[0] + LAP
-AT_FIRST_CODES = (AT_PICKED[1] + LAP, AT_PICKED[1] + LAP + 1024)
-AT_STAGE = [AT_FIRST_CODES[1] + 1024 + STAGE * i for i in range(4)]
+AT_PICKED0 = AT_WS + 4096 - LAP
+AT_PICKED = (AT_PICKED0, AT_PICKED0 + 4096)
+AT_FIRST_CODES = (AT_PICKED[0] + LAP, AT_PICKED[1])
+AT_W2 = AT_PICKED[1] + 1024
+AT_STAGE = [AT_W2 + 2048 + STAGE * i // 2 for i in (0, 2, 4, 6, 1, 8, 3)]
 AT_LATE_PLANE = AT_STAGE[3] - 256
-AT_WORDS = AT_STAGE[3] + STAGE
-AT_RAW10 = AT_WORDS
-AT_RAW11 = AT_WORDS + RAW
+AT_WORDS = AT_STAGE[5] + STAGE - LAP
+AT_RAW10 = AT_WORDS + LAP
+AT_CODES = (AT_RAW10 + RAW, AT_FIRST_CODES[0] + 1024)
+AT_RAW11 = AT_CODES[0] + 2048
 
 
 def tile_list_edge_skip_messages_kernel(
@@ -72,8 +75,6 @@ def tile_list_edge_skip_messages_kernel(
         nc.gpsimd.memset(ones[:], 1.0)
         identity = sb("identity", [P, P], F32)
         make_identity(nc, identity[:])
-        b1_cols = sb("b1_cols", [P, 2, 4], F32)
-        nc.gpsimd.dma_start(out=b1_cols[:], in_=b1.rearrange("(a p t) -> p a t", a=2, t=4))
         v_plane = [sb("v_plane%d" % g, [P, S], U8) for g in range(2)]
 
         raw = {}
@@ -110,6 +111,8 @@ def tile_list_edge_skip_messages_kernel(
 
         place_scale_rows(0)
         load_w1(0, 1, AT_RAW01)
+        b1_cols = at(AT_SCALES + LAP + 4 * N, "b1_cols", [P, 2, 4], F32)
+        nc.sync.dma_start(out=b1_cols[:], in_=b1.rearrange("(a p t) -> p a t", a=2, t=4))
         place_scale_rows(1)
         weight_planes = at(AT_SCALES + LAP, "weight_planes", [P, 2, 2 * N], U8)
         nc.vector.memset(weight_planes[:].rearrange("p w n -> p (w n)").bitcast(I32), 0)
@@ -144,19 +147,19 @@ def tile_list_edge_skip_messages_kernel(
 
         v_codes = {}
 
+        picked = {}
+
         def gather_words(half):
-            picked = at(AT_PICKED[half], "picked%d" % half, [P, HALF], U32)
+            picked[half] = at(AT_PICKED[half], "picked%d" % half, [P, HALF], U32)
             nc.vector.tensor_copy(
-                picked[:], tab_words[:].bitcast(U32).indirect(offsets[:, 32 * half : 32 * (half + 1)])
+                picked[half][:], tab_words[:].bitcast(U32).indirect(offsets[:, 32 * half : 32 * (half + 1)])
             )
-            if half == 0:
-                unread = bank(5, "unread")
-                for i in range(4):
-                    warm_up(unread, picked[:, 0:QUARTER].bitcast(FP4X4), picked_scales[:, 0:HALF], i == 0, i == 3)
-            v_codes[half] = sb("v_codes%d" % half, [P, 4 * HALF], U8)
+
+        def part_words(half, offset):
+            v_codes[half] = at(offset, "v_codes%d" % half, [P, 4 * HALF], U8)
             nc.vector.tensor_copy(
                 out=v_codes[half][:].bitcast(U16).rearrange("p (g n) -> p g n", g=2),
-                in_=picked[:].bitcast(U16).rearrange("p (n g) -> p g n", g=2),
+                in_=picked[half][:].bitcast(U16).rearrange("p (n g) -> p g n", g=2),
             )
 
         def v_operand(g, half):
@@ -173,11 +176,15 @@ def tile_list_edge_skip_messages_kernel(
 
         staged = {}
 
-        def round_w1(a, g, u, engine, slot):
+        def shared(split):
+            return [(nc.vector, 0, split), (nc.scalar, split, P)]
+
+        def round_w1(a, g, u, engines, slot):
             staged[a, g, u] = at(AT_STAGE[slot], "grouped%d%d%d" % (a, g, u), [P, 1024], BF16)
             dst = staged[a, g, u][:].rearrange("p (t m j) -> p m j t", t=2, j=4)
             src = raw[a, g][:].rearrange("p j (m t) -> p m j t", t=4)[:, :, :, 2 * u : 2 * u + 2]
-            copy_on(engine, dst, src)
+            for engine, first, last in engines:
+                copy_on(engine, dst[:, first:last], src[:, first:last])
 
         def quantize_w1(a, g, u):
             name = "w1_codes%d%d%d" % (a, g, u)
@@ -206,9 +213,10 @@ def tile_list_edge_skip_messages_kernel(
                 start=not last,
                 stop=last,
             )
-            if last:
-                if t == 0:
-                    h_rows[a, half] = sb("h_rows%d%d" % (a, half), [P, 4, HALF], BF16)
+
+        def empty_banks(a, half):
+            h_rows[a, half] = sb("h_rows%d%d" % (a, half), [P, 4, HALF], BF16)
+            for t in range(4):
                 nc.scalar.activation(
                     out=h_rows[a, half][:, t, :], in_=h_acc[half, t][:], func=ACT.Relu, bias=b1_cols[:, a, t : t + 1]
                 )
@@ -278,6 +286,14 @@ def tile_list_edge_skip_messages_kernel(
 
         for half in range(2):
             gather_words(half)
+        unread = bank(5, "unread")
+        for i in range(4):
+            moving = picked[0][:, 0:QUARTER] if i == 0 else picked_scales[:]
+            warm_up(unread, moving.bitcast(FP4X4), picked_scales[:, 0:HALF], i == 0, i == 3)
+        round_w1(0, 0, 0, shared(P // 2), 5)
+        part_words(0, AT_CODES[0])
+        quantize_w1(0, 0, 0)
+        part_words(1, AT_CODES[1])
         load_w1(1, 0, AT_RAW10)
         load_w1(1, 1, AT_RAW11)
         ws_codes = at(AT_WS, "ws_codes", [P, 2 * 4 * N], U8)
@@ -293,34 +309,44 @@ def tile_list_edge_skip_messages_kernel(
         )
         load_weight_scales(w2_plane, w2_scales)
 
-        for u in range(2):
-            round_w1(0, 0, u, nc.scalar, u)
-            quantize_w1(0, 0, u)
+        round_w1(0, 0, 1, [(nc.scalar, 0, P)], 1)
+        quantize_w1(0, 0, 1)
         b2_cols = at(AT_RAW00, "b2_cols", [P, 4], F32)
         with nc.allow_non_contiguous_dma(reason="one bias value for each partition and row tile"):
             nc.sync.dma_start(out=b2_cols[:], in_=b2.rearrange("(m p) -> p m", p=P))
-        for t in range(4):
+        for pair in range(2):
             for half in range(2):
-                first_layer(0, half, t, 0, False)
-        round_w1(0, 1, 0, nc.scalar, 2)
-        round_w1(0, 1, 1, nc.vector, 1)
+                for t in (2 * pair, 2 * pair + 1):
+                    first_layer(0, half, t, 0, False)
+        round_w1(0, 1, 0, shared(VECTOR_SHARE), 4)
+        round_w1(0, 1, 1, shared(VECTOR_SHARE), 6)
         for u in range(2):
             quantize_w1(0, 1, u)
         for half in range(2):
             for t in range(4):
                 first_layer(0, half, t, 1, True)
-        for g in range(2):
-            for u in range(2):
-                round_w1(1, g, u, nc.vector, u)
-            for u in range(2):
-                quantize_w1(1, g, u)
-        for g in range(2):
-            for t in range(4):
-                first_layer(1, 0, t, g, g == 1)
+            empty_banks(0, half)
+        for u in range(2):
+            round_w1(1, 0, u, [(nc.vector, 0, P)], u)
+        for u in range(2):
+            quantize_w1(1, 0, u)
+        for u in range(2):
+            round_w1(1, 1, u, [(nc.vector, 0, P)], 4 * u)
+            quantize_w1(1, 1, u)
         for t in range(4):
-            order = (0, 1) if t < 2 else (1, 0)
-            for g in order:
-                first_layer(1, 1, t, g, g == order[1])
+            first_layer(1, 0, t, 0, False)
+        first_layer(1, 1, 0, 0, False)
+        for t in range(2):
+            first_layer(1, 0, t, 1, True)
+        first_layer(1, 1, 0, 1, True)
+        for t in range(1, 4):
+            if t == 2:
+                for late in (2, 3):
+                    first_layer(1, 0, late, 1, True)
+            for g in (1, 0):
+                first_layer(1, 1, t, g, g == 0)
+        for half in range(2):
+            empty_banks(1, half)
         for u in range(2):
             weave_h(0, 0, u, nc.vector, u)
         for u in range(2):
@@ -345,9 +371,11 @@ def tile_list_edge_skip_messages_kernel(
             finish(m, 0)
         for pair in range(2):
             for m in (2 * pair, 2 * pair + 1):
-                output_pass("layer", 0, m, 1, start=True)
-                for g in range(2):
-                    output_pass("skip", g, m, 1)
+                steps = [("layer", 0), ("skip", 0), ("skip", 1)]
+                if m == 0:
+                    steps = steps[::-1]
+                for i, (kind, index) in enumerate(steps):
+                    output_pass(kind, index, m, 1, start=i == 0)
                 if pair == 1:
                     output_pass("layer", 1, m, 1, stop=True)
                     finish(m, 1, 2 if m == 3 else 1)

@@ -21,7 +21,7 @@ P = 128
 HALF = 512
 QUARTER = 256
 VECTOR_SHARE = 84
-LAP = 64
+LAP = 256
 RAW = 4 * 512 * 4
 STAGE = 2 * 1024
 AT_RAW00 = 0
@@ -32,12 +32,15 @@ AT_PICKED0 = AT_WS + 4096 - LAP
 AT_PICKED = (AT_PICKED0, AT_PICKED0 + 4096)
 AT_FIRST_CODES = (AT_PICKED[0] + LAP, AT_PICKED[1])
 AT_W2 = AT_PICKED[1] + 1024
-AT_STAGE = [AT_W2 + 2048 + STAGE * i // 2 for i in (0, 2, 4, 6, 1, 8, 3)]
-AT_LATE_PLANE = AT_STAGE[3] - 256
-AT_WORDS = AT_STAGE[5] + STAGE - LAP
+AT_LATE_SLOTS = AT_W2 + 2048
+AT_LATE_PLANE = AT_LATE_SLOTS + STAGE - 256
+AT_FIRST_PAIR = AT_LATE_SLOTS + 2 * STAGE
+AT_WORDS = AT_FIRST_PAIR + STAGE - LAP
 AT_RAW10 = AT_WORDS + LAP
 AT_CODES = (AT_RAW10 + RAW, AT_FIRST_CODES[0] + 1024)
-AT_RAW11 = AT_CODES[0] + 2048
+AT_SLOTS = AT_CODES[0] + 2048
+AT_RAW11 = AT_SLOTS + 2 * STAGE
+AT_STAGE = (AT_SLOTS, AT_SLOTS + STAGE, AT_LATE_SLOTS, AT_LATE_SLOTS + STAGE, AT_SLOTS + STAGE // 2, AT_FIRST_PAIR)
 
 
 def tile_list_edge_skip_messages_kernel(
@@ -50,10 +53,10 @@ def tile_list_edge_skip_messages_kernel(
         psum = ctx.enter_context(tc.psum_pool(name="psum", bufs=1))
 
         def sb(name, shape, dtype, tag=None):
-            return keep.tile(shape, dtype, name=name, tag=tag or name, align_bytes=64)
+            return keep.tile(shape, dtype, name=name, tag=tag or name, align_bytes=256)
 
         def at(offset, name, shape, dtype):
-            return land.tile(shape, dtype, name=name, offset=offset, align_bytes=64)
+            return land.tile(shape, dtype, name=name, offset=offset, align_bytes=256)
 
         def bank(b, name):
             return psum.tile([P, HALF], F32, name=name, tag="bank%d" % b)
@@ -309,7 +312,7 @@ def tile_list_edge_skip_messages_kernel(
         )
         load_weight_scales(w2_plane, w2_scales)
 
-        round_w1(0, 0, 1, [(nc.scalar, 0, P)], 1)
+        round_w1(0, 0, 1, [(nc.scalar, 0, P)], 4)
         quantize_w1(0, 0, 1)
         b2_cols = at(AT_RAW00, "b2_cols", [P, 4], F32)
         with nc.allow_non_contiguous_dma(reason="one bias value for each partition and row tile"):
@@ -318,8 +321,8 @@ def tile_list_edge_skip_messages_kernel(
             for half in range(2):
                 for t in (2 * pair, 2 * pair + 1):
                     first_layer(0, half, t, 0, False)
-        round_w1(0, 1, 0, shared(VECTOR_SHARE), 4)
-        round_w1(0, 1, 1, shared(VECTOR_SHARE), 6)
+        round_w1(0, 1, 0, shared(VECTOR_SHARE), 0)
+        round_w1(0, 1, 1, shared(VECTOR_SHARE), 1)
         for u in range(2):
             quantize_w1(0, 1, u)
         for half in range(2):

@@ -20,27 +20,35 @@ ACT = mybir.ActivationFunctionType
 P = 128
 HALF = 512
 QUARTER = 256
+WARM_UPS = 4
+TWO_ONES = 0x3F803F80
 VECTOR_SHARE = 84
-LAP = 256
+
+ALIGN = 256
 RAW = 4 * 512 * 4
 STAGE = 2 * 1024
+PAIR = 4 * 2 * P
+PLANE = 2 * N
+
 AT_RAW00 = 0
 AT_RAW01 = RAW
-AT_SCALES = 2 * RAW - LAP
+AT_SCALES = 2 * RAW - ALIGN
+AT_WEIGHT_PLANES = AT_SCALES + ALIGN
+AT_B1 = AT_WEIGHT_PLANES + 2 * PLANE
+AT_ONES = AT_B1 + ALIGN
 AT_WS = AT_SCALES + T
-AT_PICKED0 = AT_WS + 4096 - LAP
-AT_PICKED = (AT_PICKED0, AT_PICKED0 + 4096)
-AT_FIRST_CODES = (AT_PICKED[0] + LAP, AT_PICKED[1])
-AT_W2 = AT_PICKED[1] + 1024
-AT_LATE_SLOTS = AT_W2 + 2048
-AT_LATE_PLANE = AT_LATE_SLOTS + STAGE - 256
-AT_FIRST_PAIR = AT_LATE_SLOTS + 2 * STAGE
-AT_WORDS = AT_FIRST_PAIR + STAGE - LAP
-AT_RAW10 = AT_WORDS + LAP
-AT_CODES = (AT_RAW10 + RAW, AT_FIRST_CODES[0] + 1024)
-AT_SLOTS = AT_CODES[0] + 2048
-AT_RAW11 = AT_SLOTS + 2 * STAGE
-AT_STAGE = (AT_SLOTS, AT_SLOTS + STAGE, AT_LATE_SLOTS, AT_LATE_SLOTS + STAGE, AT_SLOTS + STAGE // 2, AT_FIRST_PAIR)
+AT_PICKED = (AT_WS + 2 * STAGE - ALIGN, AT_WS + 4 * STAGE - ALIGN)
+AT_FIRST_CODES = (AT_PICKED[0] + ALIGN, AT_PICKED[1])
+AT_W2 = AT_PICKED[1] + PAIR
+AT_LATE_SLOTS = (AT_W2 + STAGE, AT_W2 + 2 * STAGE)
+AT_LATE_PLANE = AT_LATE_SLOTS[1] - ALIGN
+AT_FIRST_PAIR = AT_LATE_SLOTS[1] + STAGE
+AT_WORDS = AT_FIRST_PAIR + STAGE - ALIGN
+AT_RAW10 = AT_WORDS + ALIGN
+AT_V_CODES = (AT_RAW10 + RAW, AT_FIRST_CODES[0] + PAIR)
+AT_SLOTS = (AT_V_CODES[0] + STAGE, AT_V_CODES[0] + 2 * STAGE)
+AT_ACROSS = AT_SLOTS[0] + STAGE // 2
+AT_RAW11 = AT_SLOTS[1] + STAGE
 
 
 def tile_list_edge_skip_messages_kernel(
@@ -52,11 +60,11 @@ def tile_list_edge_skip_messages_kernel(
         land = ctx.enter_context(tc.tile_pool(name="land", bufs=1))
         psum = ctx.enter_context(tc.psum_pool(name="psum", bufs=1))
 
-        def sb(name, shape, dtype, tag=None):
-            return keep.tile(shape, dtype, name=name, tag=tag or name, align_bytes=256)
+        def sb(name, shape, dtype):
+            return keep.tile(shape, dtype, name=name, tag=name, align_bytes=ALIGN)
 
         def at(offset, name, shape, dtype):
-            return land.tile(shape, dtype, name=name, offset=offset, align_bytes=256)
+            return land.tile(shape, dtype, name=name, offset=offset, align_bytes=ALIGN)
 
         def bank(b, name):
             return psum.tile([P, HALF], F32, name=name, tag="bank%d" % b)
@@ -74,8 +82,6 @@ def tile_list_edge_skip_messages_kernel(
 
         ew_cols = sb("ew_cols", [P, 8], F32)
         nc.scalar.dma_start(out=ew_cols[:], in_=ew.rearrange("(p m) -> p m", m=8))
-        ones = sb("ones", [P, 4 * P], BF16)
-        nc.gpsimd.memset(ones[:], 1.0)
         identity = sb("identity", [P, P], F32)
         make_identity(nc, identity[:])
         v_plane = [sb("v_plane%d" % g, [P, S], U8) for g in range(2)]
@@ -114,10 +120,10 @@ def tile_list_edge_skip_messages_kernel(
 
         place_scale_rows(0)
         load_w1(0, 1, AT_RAW01)
-        b1_cols = at(AT_SCALES + LAP + 4 * N, "b1_cols", [P, 2, 4], F32)
+        b1_cols = at(AT_B1, "b1_cols", [P, 2, 4], F32)
         nc.sync.dma_start(out=b1_cols[:], in_=b1.rearrange("(a p t) -> p a t", a=2, t=4))
         place_scale_rows(1)
-        weight_planes = at(AT_SCALES + LAP, "weight_planes", [P, 2, 2 * N], U8)
+        weight_planes = at(AT_WEIGHT_PLANES, "weight_planes", [P, 2, PLANE], U8)
         nc.vector.memset(weight_planes[:].rearrange("p w n -> p (w n)").bitcast(I32), 0)
         ws_plane, w2_plane = weight_planes[:, 0], weight_planes[:, 1]
 
@@ -133,24 +139,13 @@ def tile_list_edge_skip_messages_kernel(
                 func=ACT.Copy,
             )
 
+        ones = at(AT_ONES, "ones", [P, 4 * P], BF16)
+        nc.vector.memset(ones[:].bitcast(I32), TWO_ONES)
         warm_codes = sb("warm_codes", [P, P], U32)
         warm_plane = sb("warm_plane", [P, P], U8)
         nc.vector.quantize_mx(out=warm_codes[:].bitcast(FP8X4), scales=warm_plane[:], in_=ones[:])
 
-        def warm_up(acc, codes, plane, start, stop):
-            nc.tensor.matmul_mx(
-                out=acc[:],
-                lhsT=warm_codes[:].bitcast(FP8X4),
-                lhsT_scale=warm_plane[:],
-                rhs=codes,
-                rhs_scale=plane,
-                start=start,
-                stop=stop,
-            )
-
-        v_codes = {}
-
-        picked = {}
+        picked, v_codes = {}, {}
 
         def gather_words(half):
             picked[half] = at(AT_PICKED[half], "picked%d" % half, [P, HALF], U32)
@@ -158,8 +153,8 @@ def tile_list_edge_skip_messages_kernel(
                 picked[half][:], tab_words[:].bitcast(U32).indirect(offsets[:, 32 * half : 32 * (half + 1)])
             )
 
-        def part_words(half, offset):
-            v_codes[half] = at(offset, "v_codes%d" % half, [P, 4 * HALF], U8)
+        def part_words(half):
+            v_codes[half] = at(AT_V_CODES[half], "v_codes%d" % half, [P, 4 * HALF], U8)
             nc.vector.tensor_copy(
                 out=v_codes[half][:].bitcast(U16).rearrange("p (g n) -> p g n", g=2),
                 in_=picked[half][:].bitcast(U16).rearrange("p (n g) -> p g n", g=2),
@@ -175,19 +170,15 @@ def tile_list_edge_skip_messages_kernel(
             else:
                 nc.scalar.copy(out=dst, in_=src)
 
-        w1_codes, w1_plane = {}, {}
+        staged, w1_codes, w1_plane = {}, {}, {}
 
-        staged = {}
-
-        def shared(split):
-            return [(nc.vector, 0, split), (nc.scalar, split, P)]
-
-        def round_w1(a, g, u, engines, slot):
-            staged[a, g, u] = at(AT_STAGE[slot], "grouped%d%d%d" % (a, g, u), [P, 1024], BF16)
+        def round_w1(a, g, u, split, offset):
+            staged[a, g, u] = at(offset, "staged%d%d%d" % (a, g, u), [P, 1024], BF16)
             dst = staged[a, g, u][:].rearrange("p (t m j) -> p m j t", t=2, j=4)
             src = raw[a, g][:].rearrange("p j (m t) -> p m j t", t=4)[:, :, :, 2 * u : 2 * u + 2]
-            for engine, first, last in engines:
-                copy_on(engine, dst[:, first:last], src[:, first:last])
+            for engine, first, last in ((nc.vector, 0, split), (nc.scalar, split, P)):
+                if first < last:
+                    copy_on(engine, dst[:, first:last], src[:, first:last])
 
         def quantize_w1(a, g, u):
             name = "w1_codes%d%d%d" % (a, g, u)
@@ -200,10 +191,10 @@ def tile_list_edge_skip_messages_kernel(
                 out=w1_codes[a, g, u][:].bitcast(FP8X4), scales=w1_plane[a, g, u][:], in_=staged[a, g, u][:]
             )
 
-        h_rows, h_codes, h_plane, h_acc = {}, {}, {}, {}
+        h_acc, h_rows, woven, h_codes, h_plane = {}, {}, {}, {}, {}
 
-        def first_layer(a, half, t, g, last):
-            if not last:
+        def first_layer(a, half, t, g, closes):
+            if not closes:
                 h_acc[half, t] = bank(4 * half + t, "h_acc")
             cols = slice(P * (t % 2), P * (t % 2 + 1))
             codes, plane = v_operand(g, half)
@@ -213,8 +204,8 @@ def tile_list_edge_skip_messages_kernel(
                 lhsT_scale=w1_plane[a, g, t // 2][:, cols],
                 rhs=codes,
                 rhs_scale=plane,
-                start=not last,
-                stop=last,
+                start=not closes,
+                stop=closes,
             )
 
         def empty_banks(a, half):
@@ -224,20 +215,16 @@ def tile_list_edge_skip_messages_kernel(
                     out=h_rows[a, half][:, t, :], in_=h_acc[half, t][:], func=ACT.Relu, bias=b1_cols[:, a, t : t + 1]
                 )
 
-        woven = {}
-
-        def weave_h(a, half, u, engine, slot=None):
+        def weave_h(a, half, u, engine, offset=None):
             name = "h_woven%d%d%d" % (a, half, u)
-            if engine is nc.vector:
-                woven[a, half, u] = at(AT_STAGE[slot], name, [P, 4 * QUARTER], BF16)
-            else:
-                woven[a, half, u] = sb(name, [P, 4 * QUARTER], BF16)
+            shape = [P, 4 * QUARTER]
+            woven[a, half, u] = sb(name, shape, BF16) if offset is None else at(offset, name, shape, BF16)
             dst = woven[a, half, u][:].rearrange("p (c i t) -> p c t i", i=4, t=4)
             src = h_rows[a, half][:, :, QUARTER * u : QUARTER * (u + 1)].rearrange("p t (c i) -> p c t i", i=4)
             copy_on(engine, dst, src)
 
         def quantize_h(a, half, u):
-            if (a, half) not in h_codes:
+            if u == 0:
                 h_codes[a, half] = sb("h_codes%d%d" % (a, half), [P, HALF], U32)
                 if (a, half) == (0, 1):
                     h_plane[a, half] = at(AT_LATE_PLANE, "h_plane01", [P, HALF], U8)
@@ -289,14 +276,24 @@ def tile_list_edge_skip_messages_kernel(
 
         for half in range(2):
             gather_words(half)
+
         unread = bank(5, "unread")
-        for i in range(4):
+        for i in range(WARM_UPS):
             moving = picked[0][:, 0:QUARTER] if i == 0 else picked_scales[:]
-            warm_up(unread, moving.bitcast(FP4X4), picked_scales[:, 0:HALF], i == 0, i == 3)
-        round_w1(0, 0, 0, shared(P // 2), 5)
-        part_words(0, AT_CODES[0])
+            nc.tensor.matmul_mx(
+                out=unread[:],
+                lhsT=warm_codes[:].bitcast(FP8X4),
+                lhsT_scale=warm_plane[:],
+                rhs=moving.bitcast(FP4X4),
+                rhs_scale=picked_scales[:, 0:HALF],
+                start=i == 0,
+                stop=i == WARM_UPS - 1,
+            )
+
+        round_w1(0, 0, 0, P // 2, AT_FIRST_PAIR)
+        part_words(0)
         quantize_w1(0, 0, 0)
-        part_words(1, AT_CODES[1])
+        part_words(1)
         load_w1(1, 0, AT_RAW10)
         load_w1(1, 1, AT_RAW11)
         ws_codes = at(AT_WS, "ws_codes", [P, 2 * 4 * N], U8)
@@ -312,58 +309,61 @@ def tile_list_edge_skip_messages_kernel(
         )
         load_weight_scales(w2_plane, w2_scales)
 
-        round_w1(0, 0, 1, [(nc.scalar, 0, P)], 4)
+        round_w1(0, 0, 1, 0, AT_ACROSS)
         quantize_w1(0, 0, 1)
         b2_cols = at(AT_RAW00, "b2_cols", [P, 4], F32)
         with nc.allow_non_contiguous_dma(reason="one bias value for each partition and row tile"):
             nc.sync.dma_start(out=b2_cols[:], in_=b2.rearrange("(m p) -> p m", p=P))
-        for pair in range(2):
+        for u in range(2):
             for half in range(2):
-                for t in (2 * pair, 2 * pair + 1):
+                for t in (2 * u, 2 * u + 1):
                     first_layer(0, half, t, 0, False)
-        round_w1(0, 1, 0, shared(VECTOR_SHARE), 0)
-        round_w1(0, 1, 1, shared(VECTOR_SHARE), 1)
+        for u in range(2):
+            round_w1(0, 1, u, VECTOR_SHARE, AT_SLOTS[u])
         for u in range(2):
             quantize_w1(0, 1, u)
         for half in range(2):
             for t in range(4):
                 first_layer(0, half, t, 1, True)
             empty_banks(0, half)
+
         for u in range(2):
-            round_w1(1, 0, u, [(nc.vector, 0, P)], u)
+            round_w1(1, 0, u, P, AT_SLOTS[u])
         for u in range(2):
             quantize_w1(1, 0, u)
-        for u in range(2):
-            round_w1(1, 1, u, [(nc.vector, 0, P)], 4 * u)
+        for u, offset in enumerate((AT_SLOTS[0], AT_ACROSS)):
+            round_w1(1, 1, u, P, offset)
             quantize_w1(1, 1, u)
         for t in range(4):
             first_layer(1, 0, t, 0, False)
         first_layer(1, 1, 0, 0, False)
-        for t in range(2):
+        for half, t in ((0, 0), (0, 1), (1, 0)):
+            first_layer(1, half, t, 1, True)
+        for g in (1, 0):
+            first_layer(1, 1, 1, g, g == 0)
+        for t in (2, 3):
             first_layer(1, 0, t, 1, True)
-        first_layer(1, 1, 0, 1, True)
-        for t in range(1, 4):
-            if t == 2:
-                for late in (2, 3):
-                    first_layer(1, 0, late, 1, True)
+        for t in (2, 3):
             for g in (1, 0):
                 first_layer(1, 1, t, g, g == 0)
         for half in range(2):
             empty_banks(1, half)
+
         for u in range(2):
-            weave_h(0, 0, u, nc.vector, u)
+            weave_h(0, 0, u, nc.vector, AT_SLOTS[u])
         for u in range(2):
             quantize_h(0, 0, u)
         for u in range(2):
-            weave_h(0, 1, u, nc.vector, u)
+            weave_h(0, 1, u, nc.vector, AT_SLOTS[u])
         for u in range(2):
-            weave_h(1, 0, u, nc.vector, 2 + u)
+            weave_h(1, 0, u, nc.vector, AT_LATE_SLOTS[u])
         for a, half in ((1, 0), (0, 1)):
             for u in range(2):
                 quantize_h(a, half, u)
         for u in range(2):
             weave_h(1, 1, u, nc.scalar)
             quantize_h(1, 1, u)
+
         for m in range(4):
             for g in range(2):
                 output_pass("skip", g, m, 0, start=g == 0)
@@ -372,17 +372,21 @@ def tile_list_edge_skip_messages_kernel(
                 output_pass("layer", a, m, 0, stop=a == 1)
         for m in range(4):
             finish(m, 0)
-        for pair in range(2):
-            for m in (2 * pair, 2 * pair + 1):
-                steps = [("layer", 0), ("skip", 0), ("skip", 1)]
-                if m == 0:
-                    steps = steps[::-1]
-                for i, (kind, index) in enumerate(steps):
-                    output_pass(kind, index, m, 1, start=i == 0)
-                if pair == 1:
-                    output_pass("layer", 1, m, 1, stop=True)
-                    finish(m, 1, 2 if m == 3 else 1)
-            if pair == 0:
-                for m in range(2):
-                    output_pass("layer", 1, m, 1, stop=True)
-                    finish(m, 1)
+
+        opening = (("layer", 0), ("skip", 0), ("skip", 1))
+
+        def open_tile(m):
+            for i, (kind, index) in enumerate(opening[::-1] if m == 0 else opening):
+                output_pass(kind, index, m, 1, start=i == 0)
+
+        def close_tile(m):
+            output_pass("layer", 1, m, 1, stop=True)
+            finish(m, 1, 2 if m == 3 else 1)
+
+        for m in range(2):
+            open_tile(m)
+        for m in range(2):
+            close_tile(m)
+        for m in (2, 3):
+            open_tile(m)
+            close_tile(m)

@@ -21,15 +21,16 @@ P = 128
 HALF = 512
 QUARTER = 256
 WARM_UPS = 4
+FILLERS = 2
 TWO_ONES = 0x3F803F80
-VECTOR_SHARE = 84
+FIRST_SHARE = 32
 
 ALIGN = 256
 RAW = 4 * 512 * 4
 STAGE = 2 * 1024
-PAIR = 4 * 2 * P
 PLANE = 2 * N
 
+KIB = 1024
 AT_RAW00 = 0
 AT_RAW01 = RAW
 AT_SCALES = 2 * RAW - ALIGN
@@ -37,18 +38,15 @@ AT_WEIGHT_PLANES = AT_SCALES + ALIGN
 AT_B1 = AT_WEIGHT_PLANES + 2 * PLANE
 AT_ONES = AT_B1 + ALIGN
 AT_WS = AT_SCALES + T
-AT_PICKED = (AT_WS + 2 * STAGE - ALIGN, AT_WS + 4 * STAGE - ALIGN)
-AT_FIRST_CODES = (AT_PICKED[0] + ALIGN, AT_PICKED[1])
-AT_W2 = AT_PICKED[1] + PAIR
-AT_LATE_SLOTS = (AT_W2 + STAGE, AT_W2 + 2 * STAGE)
-AT_LATE_PLANE = AT_LATE_SLOTS[1] - ALIGN
-AT_FIRST_PAIR = AT_LATE_SLOTS[1] + STAGE
-AT_WORDS = AT_FIRST_PAIR + STAGE - ALIGN
-AT_RAW10 = AT_WORDS + ALIGN
-AT_V_CODES = (AT_RAW10 + RAW, AT_FIRST_CODES[0] + PAIR)
-AT_SLOTS = (AT_V_CODES[0] + STAGE, AT_V_CODES[0] + 2 * STAGE)
-AT_ACROSS = AT_SLOTS[0] + STAGE // 2
-AT_RAW11 = AT_SLOTS[1] + STAGE
+AT_PICKED = (AT_WS + 2 * STAGE - ALIGN, AT_WS + 3 * STAGE - ALIGN)
+AT_W2 = AT_PICKED[1] + ALIGN
+AT_WORDS = AT_W2 + STAGE
+AT_RAW10 = AT_WORDS
+AT_RAW11 = AT_WORDS + RAW
+AT_STAIRS = AT_WORDS + 4 * T
+AT_SLOT_B = AT_STAIRS + 3 * STAGE
+AT_LATE_SLOTS = (AT_SLOT_B + STAGE, AT_SLOT_B + 2 * STAGE)
+AT_FIRST_SLOT = AT_LATE_SLOTS[1] + STAGE
 
 
 def tile_list_edge_skip_messages_kernel(
@@ -77,6 +75,13 @@ def tile_list_edge_skip_messages_kernel(
                     in_=scales[:, 4 * q : 4 * q + 4, :].rearrange("a r n -> r a n").bitcast(I32),
                 )
 
+        raw = {}
+
+        def load_w1(a, g, offset):
+            raw[a, g] = at(offset, "raw%d%d" % (a, g), [P, 4, 512], F32)
+            rows = w1[512 * g : 512 * (g + 1), 512 * a : 512 * (a + 1)].rearrange("(p j) c -> p j c", j=4)
+            nc.sync.dma_start(out=raw[a, g][:], in_=rows)
+
         offsets = keep.tile([P, S // 16], U16, name="offsets")
         nc.sync.dma_start(offsets[:], offs)
 
@@ -85,13 +90,6 @@ def tile_list_edge_skip_messages_kernel(
         identity = sb("identity", [P, P], F32)
         make_identity(nc, identity[:])
         v_plane = [sb("v_plane%d" % g, [P, S], U8) for g in range(2)]
-
-        raw = {}
-
-        def load_w1(a, g, offset):
-            raw[a, g] = at(offset, "raw%d%d" % (a, g), [P, 4, 512], F32)
-            rows = w1[512 * g : 512 * (g + 1), 512 * a : 512 * (a + 1)].rearrange("(p j) c -> p j c", j=4)
-            nc.sync.dma_start(out=raw[a, g][:], in_=rows)
 
         word_bytes = 512 * T
         tab_scales = at(AT_SCALES, "tab_scales", [P, T], U8)
@@ -145,25 +143,6 @@ def tile_list_edge_skip_messages_kernel(
         warm_plane = sb("warm_plane", [P, P], U8)
         nc.vector.quantize_mx(out=warm_codes[:].bitcast(FP8X4), scales=warm_plane[:], in_=ones[:])
 
-        picked, v_codes = {}, {}
-
-        def gather_words(half):
-            picked[half] = at(AT_PICKED[half], "picked%d" % half, [P, HALF], U32)
-            nc.vector.tensor_copy(
-                picked[half][:], tab_words[:].bitcast(U32).indirect(offsets[:, 32 * half : 32 * (half + 1)])
-            )
-
-        def part_words(half):
-            v_codes[half] = at(AT_V_CODES[half], "v_codes%d" % half, [P, 4 * HALF], U8)
-            nc.vector.tensor_copy(
-                out=v_codes[half][:].bitcast(U16).rearrange("p (g n) -> p g n", g=2),
-                in_=picked[half][:].bitcast(U16).rearrange("p (n g) -> p g n", g=2),
-            )
-
-        def v_operand(g, half):
-            codes = v_codes[half][:, 2 * HALF * g : 2 * HALF * (g + 1)].bitcast(FP4X4)
-            return codes, v_plane[g][:, HALF * half : HALF * (half + 1)]
-
         def copy_on(engine, dst, src):
             if engine is nc.vector:
                 nc.vector.tensor_copy(out=dst, in_=src)
@@ -172,24 +151,42 @@ def tile_list_edge_skip_messages_kernel(
 
         staged, w1_codes, w1_plane = {}, {}, {}
 
-        def round_w1(a, g, u, split, offset):
+        def stage(a, g, u, offset):
             staged[a, g, u] = at(offset, "staged%d%d%d" % (a, g, u), [P, 1024], BF16)
+
+        def round_w1(engine, a, g, u, first=0, last=P):
             dst = staged[a, g, u][:].rearrange("p (t m j) -> p m j t", t=2, j=4)
             src = raw[a, g][:].rearrange("p j (m t) -> p m j t", t=4)[:, :, :, 2 * u : 2 * u + 2]
-            for engine, first, last in ((nc.vector, 0, split), (nc.scalar, split, P)):
-                if first < last:
-                    copy_on(engine, dst[:, first:last], src[:, first:last])
+            copy_on(engine, dst[:, first:last], src[:, first:last])
 
         def quantize_w1(a, g, u):
-            name = "w1_codes%d%d%d" % (a, g, u)
-            if (a, g) == (0, 0):
-                w1_codes[a, g, u] = at(AT_FIRST_CODES[u], name, [P, 2 * P], U32)
-            else:
-                w1_codes[a, g, u] = sb(name, [P, 2 * P], U32)
+            w1_codes[a, g, u] = sb("w1_codes%d%d%d" % (a, g, u), [P, 2 * P], U32)
             w1_plane[a, g, u] = sb("w1_plane%d%d%d" % (a, g, u), [P, 2 * P], U8)
             nc.vector.quantize_mx(
                 out=w1_codes[a, g, u][:].bitcast(FP8X4), scales=w1_plane[a, g, u][:], in_=staged[a, g, u][:]
             )
+
+        picked = [at(AT_PICKED[half], "picked%d" % half, [P, HALF], U32) for half in range(2)]
+        v_codes = {}
+
+        def gather_words(first, count):
+            half, column = divmod(first, HALF)
+            nc.vector.tensor_copy(
+                picked[half][:, column : column + count],
+                tab_words[:].bitcast(U32).indirect(offsets[:, first // 16 : (first + count) // 16]),
+            )
+
+        def part_words(half, g, offset=None):
+            name = "v_codes%d%d" % (half, g)
+            shape = [P, 2 * HALF]
+            v_codes[half, g] = sb(name, shape, U8) if offset is None else at(offset, name, shape, U8)
+            nc.vector.tensor_copy(
+                out=v_codes[half, g][:].bitcast(U16),
+                in_=picked[half][:].bitcast(U16).rearrange("p (n g) -> p g n", g=2)[:, g],
+            )
+
+        def v_operand(g, half):
+            return v_codes[half, g][:].bitcast(FP4X4), v_plane[g][:, HALF * half : HALF * (half + 1)]
 
         h_acc, h_rows, woven, h_codes, h_plane = {}, {}, {}, {}, {}
 
@@ -223,13 +220,11 @@ def tile_list_edge_skip_messages_kernel(
             src = h_rows[a, half][:, :, QUARTER * u : QUARTER * (u + 1)].rearrange("p t (c i) -> p c t i", i=4)
             copy_on(engine, dst, src)
 
-        def quantize_h(a, half, u):
+        def quantize_h(a, half, u, offset=None):
             if u == 0:
                 h_codes[a, half] = sb("h_codes%d%d" % (a, half), [P, HALF], U32)
-                if (a, half) == (0, 1):
-                    h_plane[a, half] = at(AT_LATE_PLANE, "h_plane01", [P, HALF], U8)
-                else:
-                    h_plane[a, half] = sb("h_plane%d%d" % (a, half), [P, HALF], U8)
+                name = "h_plane%d%d" % (a, half)
+                h_plane[a, half] = sb(name, [P, HALF], U8) if offset is None else at(offset, name, [P, HALF], U8)
             cols = slice(QUARTER * u, QUARTER * (u + 1))
             nc.vector.quantize_mx(
                 out=h_codes[a, half][:, cols].bitcast(FP8X4), scales=h_plane[a, half][:, cols], in_=woven[a, half, u][:]
@@ -273,9 +268,10 @@ def tile_list_edge_skip_messages_kernel(
                     op1=ALU.mult,
                 )
                 nc.sync.dma_start(out=out[P * m : P * (m + 1), cols], in_=result[:])
+            return result
 
         for half in range(2):
-            gather_words(half)
+            gather_words(HALF * half, HALF)
 
         unread = bank(5, "unread")
         for i in range(WARM_UPS):
@@ -290,10 +286,23 @@ def tile_list_edge_skip_messages_kernel(
                 stop=i == WARM_UPS - 1,
             )
 
-        round_w1(0, 0, 0, P // 2, AT_FIRST_PAIR)
-        part_words(0)
-        quantize_w1(0, 0, 0)
-        part_words(1)
+        for g in range(2):
+            for half in range(2):
+                part_words(half, g)
+        stage(0, 0, 0, AT_STAIRS)
+        round_w1(nc.scalar, 0, 0, 0)
+        stage(0, 0, 1, AT_FIRST_SLOT)
+        round_w1(nc.vector, 0, 0, 1, 0, FIRST_SHARE)
+        round_w1(nc.scalar, 0, 0, 1, FIRST_SHARE, P)
+        for u in range(2):
+            quantize_w1(0, 0, u)
+        stage(0, 1, 0, AT_STAIRS + KIB)
+        round_w1(nc.vector, 0, 1, 0)
+        stage(0, 1, 1, AT_SLOT_B)
+        round_w1(nc.scalar, 0, 1, 1)
+        for u in range(2):
+            quantize_w1(0, 1, u)
+
         load_w1(1, 0, AT_RAW10)
         load_w1(1, 1, AT_RAW11)
         ws_codes = at(AT_WS, "ws_codes", [P, 2 * 4 * N], U8)
@@ -309,38 +318,46 @@ def tile_list_edge_skip_messages_kernel(
         )
         load_weight_scales(w2_plane, w2_scales)
 
-        round_w1(0, 0, 1, 0, AT_ACROSS)
-        quantize_w1(0, 0, 1)
         b2_cols = at(AT_RAW00, "b2_cols", [P, 4], F32)
         with nc.allow_non_contiguous_dma(reason="one bias value for each partition and row tile"):
             nc.sync.dma_start(out=b2_cols[:], in_=b2.rearrange("(m p) -> p m", p=P))
-        for u in range(2):
-            for half in range(2):
-                for t in (2 * u, 2 * u + 1):
-                    first_layer(0, half, t, 0, False)
-        for u in range(2):
-            round_w1(0, 1, u, VECTOR_SHARE, AT_SLOTS[u])
-        for u in range(2):
-            quantize_w1(0, 1, u)
-        for half in range(2):
-            for t in range(4):
-                first_layer(0, half, t, 1, True)
-            empty_banks(0, half)
 
-        for u in range(2):
-            round_w1(1, 0, u, P, AT_SLOTS[u])
+        for half in range(2):
+            for t in range(2):
+                first_layer(0, half, t, 0, False)
+        first_layer(0, 0, 2, 0, False)
+        for t in range(3):
+            first_layer(0, 0, t, 1, True)
+        for g in (1, 0):
+            first_layer(0, 0, 3, g, g == 0)
+        empty_banks(0, 0)
+        for t in range(2):
+            first_layer(0, 1, t, 1, True)
+        for t in (2, 3):
+            for g in (1, 0):
+                first_layer(0, 1, t, g, g == 0)
+        empty_banks(0, 1)
+
+        for u, offset in enumerate((AT_STAIRS + 2 * KIB, AT_SLOT_B)):
+            stage(1, 0, u, offset)
+            round_w1(nc.vector, 1, 0, u)
         for u in range(2):
             quantize_w1(1, 0, u)
-        for u, offset in enumerate((AT_SLOTS[0], AT_ACROSS)):
-            round_w1(1, 1, u, P, offset)
-            quantize_w1(1, 1, u)
+        stage(1, 1, 0, AT_STAIRS + 3 * KIB)
+        round_w1(nc.vector, 1, 1, 0)
+        stage(1, 1, 1, AT_SLOT_B)
+        round_w1(nc.vector, 1, 1, 1, 0, P // 2)
+        quantize_w1(1, 1, 0)
+        round_w1(nc.vector, 1, 1, 1, P // 2, P)
+        weave_h(0, 0, 0, nc.vector, AT_STAIRS + 2 * KIB)
+        quantize_w1(1, 1, 1)
         for t in range(4):
             first_layer(1, 0, t, 0, False)
-        first_layer(1, 1, 0, 0, False)
-        for half, t in ((0, 0), (0, 1), (1, 0)):
-            first_layer(1, half, t, 1, True)
-        for g in (1, 0):
-            first_layer(1, 1, 1, g, g == 0)
+        for t in range(FILLERS):
+            first_layer(1, 1, t, 0, False)
+        for half in range(2):
+            for t in range(2):
+                first_layer(1, half, t, 1, True)
         for t in (2, 3):
             first_layer(1, 0, t, 1, True)
         for t in (2, 3):
@@ -349,17 +366,17 @@ def tile_list_edge_skip_messages_kernel(
         for half in range(2):
             empty_banks(1, half)
 
-        for u in range(2):
-            weave_h(0, 0, u, nc.vector, AT_SLOTS[u])
+        weave_h(0, 0, 1, nc.vector, AT_STAIRS + 4 * KIB)
         for u in range(2):
             quantize_h(0, 0, u)
         for u in range(2):
-            weave_h(0, 1, u, nc.vector, AT_SLOTS[u])
+            weave_h(0, 1, u, nc.vector, AT_STAIRS + (2 + 2 * u) * KIB)
         for u in range(2):
             weave_h(1, 0, u, nc.vector, AT_LATE_SLOTS[u])
-        for a, half in ((1, 0), (0, 1)):
-            for u in range(2):
-                quantize_h(a, half, u)
+        for u in range(2):
+            quantize_h(1, 0, u)
+        for u in range(2):
+            quantize_h(0, 1, u, AT_LATE_SLOTS[0])
         for u in range(2):
             weave_h(1, 1, u, nc.scalar)
             quantize_h(1, 1, u)

from contextlib import ExitStack

import concourse.mybir as mybir
from concourse.masks import make_identity

K, T, S, H, N = 1024, 4096, 1024, 1024, 512
FLOPS = 2 * S * (K * H + H * N + K * N)

F32 = mybir.dt.float32
BF16 = mybir.dt.bfloat16
I32 = mybir.dt.int32
U32 = mybir.dt.uint32
U16 = mybir.dt.uint16
U8 = mybir.dt.uint8
FP8X4 = mybir.dt.float8_e4m3fn_x4
FP4X4 = mybir.dt.float4_e2m1fn_x4
ALU = mybir.AluOpType
ACT = mybir.ActivationFunctionType

P = 128
HALF = 512
QUARTER = 256
WARM_UPS = 4
FILLERS = 2
TWO_ONES = 0x3F803F80
FIRST_SHARE = 32

ALIGN = 256
RAW = 4 * 512 * 4
STAGE = 2 * 1024
PLANE = 2 * N

KIB = 1024
AT_RAW00 = 0
AT_RAW01 = RAW
AT_SCALES = 2 * RAW - ALIGN
AT_WEIGHT_PLANES = AT_SCALES + ALIGN
AT_B1 = AT_WEIGHT_PLANES + 2 * PLANE
AT_ONES = AT_B1 + ALIGN
AT_WS = AT_SCALES + T
AT_PICKED = (AT_WS + 2 * STAGE - ALIGN, AT_WS + 3 * STAGE - ALIGN)
AT_W2 = AT_PICKED[1] + ALIGN
AT_WORDS = AT_W2 + STAGE
AT_RAW10 = AT_WORDS
AT_RAW11 = AT_WORDS + RAW
AT_STAIRS = AT_WORDS + 4 * T
AT_SLOT_B = AT_STAIRS + 3 * STAGE
AT_LATE_SLOTS = (AT_SLOT_B + STAGE, AT_SLOT_B + 2 * STAGE)
AT_FIRST_SLOT = AT_LATE_SLOTS[1] + STAGE


def tile_list_edge_skip_messages_kernel(
    tc, tab, offs, w1, b1, w2_words, w2_scales, ws_words, ws_scales, b2, ew, out
):
    nc = tc.nc
    with ExitStack() as ctx:
        keep = ctx.enter_context(tc.tile_pool(name="keep", bufs=1))
        land = ctx.enter_context(tc.tile_pool(name="land", bufs=1))
        psum = ctx.enter_context(tc.psum_pool(name="psum", bufs=1))

        def sb(name, shape, dtype):
            return keep.tile(shape, dtype, name=name, tag=name, align_bytes=ALIGN)

        def at(offset, name, shape, dtype):
            return land.tile(shape, dtype, name=name, offset=offset, align_bytes=ALIGN)

        def bank(b, name):
            return psum.tile([P, HALF], F32, name=name, tag="bank%d" % b)

        def load_weight_scales(plane, scales):
            rows = plane.bitcast(I32).rearrange("p (a n) -> p a n", a=2)
            for q in range(4):
                nc.sync.dma_start(
                    out=rows[32 * q : 32 * q + 4],
                    in_=scales[:, 4 * q : 4 * q + 4, :].rearrange("a r n -> r a n").bitcast(I32),
                )

        raw = {}

        def load_w1(a, g, offset):
            raw[a, g] = at(offset, "raw%d%d" % (a, g), [P, 4, 512], F32)
            rows = w1[512 * g : 512 * (g + 1), 512 * a : 512 * (a + 1)].rearrange("(p j) c -> p j c", j=4)
            nc.sync.dma_start(out=raw[a, g][:], in_=rows)

        offsets = keep.tile([P, S // 16], U16, name="offsets")
        nc.sync.dma_start(offsets[:], offs)

        ew_cols = sb("ew_cols", [P, 8], F32)
        nc.scalar.dma_start(out=ew_cols[:], in_=ew.rearrange("(p m) -> p m", m=8))
        identity = sb("identity", [P, P], F32)
        make_identity(nc, identity[:])
        v_plane = [sb("v_plane%d" % g, [P, S], U8) for g in range(2)]

        word_bytes = 512 * T
        tab_scales = at(AT_SCALES, "tab_scales", [P, T], U8)
        nc.sync.dma_start(
            out=tab_scales[:].bitcast(I32)[0:32, :],
            in_=tab[0, word_bytes:].rearrange("(i b) -> i b", i=32).bitcast(I32),
        )
        nc.vector.memset(tab_scales[:].bitcast(I32)[64:P, :], 0)
        nc.vector.memset(tab_scales[:].bitcast(I32)[32:64, :], 0)
        tab_words = at(AT_WORDS, "tab_words", [P, T], I32)
        nc.sync.dma_start(out=tab_words[:], in_=tab[0, 0:word_bytes].rearrange("(p b) -> p b", p=P).bitcast(I32))
        load_w1(0, 0, AT_RAW00)

        for plane in v_plane:
            nc.vector.memset(plane[:].bitcast(I32), 0)
        picked_scales = sb("picked_scales", [P, S], U8)
        nc.vector.tensor_copy(picked_scales[:], tab_scales[:].indirect(offsets[:]))

        def place_scale_rows(g):
            for q in range(4):
                first = 16 * g + 4 * q
                nc.sync.dma_start(
                    out=v_plane[g][:].bitcast(I32)[32 * q : 32 * q + 4, :],
                    in_=picked_scales[:].bitcast(I32)[first : first + 4, :],
                )

        place_scale_rows(0)
        load_w1(0, 1, AT_RAW01)
        b1_cols = at(AT_B1, "b1_cols", [P, 2, 4], F32)
        nc.sync.dma_start(out=b1_cols[:], in_=b1.rearrange("(a p t) -> p a t", a=2, t=4))
        place_scale_rows(1)
        weight_planes = at(AT_WEIGHT_PLANES, "weight_planes", [P, 2, PLANE], U8)
        nc.vector.memset(weight_planes[:].rearrange("p w n -> p (w n)").bitcast(I32), 0)
        ws_plane, w2_plane = weight_planes[:, 0], weight_planes[:, 1]

        edge_weight = sb("edge_weight", [P, S], F32)
        for i in range(2):
            spread = bank(4 + i, "spread")
            for m in range(4):
                column = ew_cols[:, 4 * i + m : 4 * i + m + 1].to_broadcast([P, P])
                nc.tensor.transpose(spread[:, P * m : P * (m + 1)], column, identity[:])
            nc.scalar.activation(
                out=edge_weight[:].rearrange("p (n i m) -> p i n m", i=2, m=4)[:, i],
                in_=spread[:].rearrange("p (m n) -> p n m", m=4),
                func=ACT.Copy,
            )

        ones = at(AT_ONES, "ones", [P, 4 * P], BF16)
        nc.vector.memset(ones[:].bitcast(I32), TWO_ONES)
        warm_codes = sb("warm_codes", [P, P], U32)
        warm_plane = sb("warm_plane", [P, P], U8)
        nc.vector.quantize_mx(out=warm_codes[:].bitcast(FP8X4), scales=warm_plane[:], in_=ones[:])

        def copy_on(engine, dst, src):
            if engine is nc.vector:
                nc.vector.tensor_copy(out=dst, in_=src)
            else:
                nc.scalar.copy(out=dst, in_=src)

        staged, w1_codes, w1_plane = {}, {}, {}

        def stage(a, g, u, offset):
            staged[a, g, u] = at(offset, "staged%d%d%d" % (a, g, u), [P, 1024], BF16)

        def round_w1(engine, a, g, u, first=0, last=P):
            dst = staged[a, g, u][:].rearrange("p (t m j) -> p m j t", t=2, j=4)
            src = raw[a, g][:].rearrange("p j (m t) -> p m j t", t=4)[:, :, :, 2 * u : 2 * u + 2]
            copy_on(engine, dst[:, first:last], src[:, first:last])

        def quantize_w1(a, g, u):
            w1_codes[a, g, u] = sb("w1_codes%d%d%d" % (a, g, u), [P, 2 * P], U32)
            w1_plane[a, g, u] = sb("w1_plane%d%d%d" % (a, g, u), [P, 2 * P], U8)
            nc.vector.quantize_mx(
                out=w1_codes[a, g, u][:].bitcast(FP8X4), scales=w1_plane[a, g, u][:], in_=staged[a, g, u][:]
            )

        picked = [at(AT_PICKED[half], "picked%d" % half, [P, HALF], U32) for half in range(2)]
        v_codes = {}

        def gather_words(first, count):
            half, column = divmod(first, HALF)
            nc.vector.tensor_copy(
                picked[half][:, column : column + count],
                tab_words[:].bitcast(U32).indirect(offsets[:, first // 16 : (first + count) // 16]),
            )

        def part_words(half, g, offset=None):
            name = "v_codes%d%d" % (half, g)
            shape = [P, 2 * HALF]
            v_codes[half, g] = sb(name, shape, U8) if offset is None else at(offset, name, shape, U8)
            nc.vector.tensor_copy(
                out=v_codes[half, g][:].bitcast(U16),
                in_=picked[half][:].bitcast(U16).rearrange("p (n g) -> p g n", g=2)[:, g],
            )

        def v_operand(g, half):
            return v_codes[half, g][:].bitcast(FP4X4), v_plane[g][:, HALF * half : HALF * (half + 1)]

        h_acc, h_rows, woven, h_codes, h_plane = {}, {}, {}, {}, {}

        def first_layer(a, half, t, g, closes):
            if not closes:
                h_acc[half, t] = bank(4 * half + t, "h_acc")
            cols = slice(P * (t % 2), P * (t % 2 + 1))
            codes, plane = v_operand(g, half)
            nc.tensor.matmul_mx(
                out=h_acc[half, t][:],
                lhsT=w1_codes[a, g, t // 2][:, cols].bitcast(FP8X4),
                lhsT_scale=w1_plane[a, g, t // 2][:, cols],
                rhs=codes,
                rhs_scale=plane,
                start=not closes,
                stop=closes,
            )

        def empty_banks(a, half):
            h_rows[a, half] = sb("h_rows%d%d" % (a, half), [P, 4, HALF], BF16)
            for t in range(4):
                nc.scalar.activation(
                    out=h_rows[a, half][:, t, :], in_=h_acc[half, t][:], func=ACT.Relu, bias=b1_cols[:, a, t : t + 1]
                )

        def weave_h(a, half, u, engine, offset=None):
            name = "h_woven%d%d%d" % (a, half, u)
            shape = [P, 4 * QUARTER]
            woven[a, half, u] = sb(name, shape, BF16) if offset is None else at(offset, name, shape, BF16)
            dst = woven[a, half, u][:].rearrange("p (c i t) -> p c t i", i=4, t=4)
            src = h_rows[a, half][:, :, QUARTER * u : QUARTER * (u + 1)].rearrange("p t (c i) -> p c t i", i=4)
            copy_on(engine, dst, src)

        def quantize_h(a, half, u, offset=None):
            if u == 0:
                h_codes[a, half] = sb("h_codes%d%d" % (a, half), [P, HALF], U32)
                name = "h_plane%d%d" % (a, half)
                h_plane[a, half] = sb(name, [P, HALF], U8) if offset is None else at(offset, name, [P, HALF], U8)
            cols = slice(QUARTER * u, QUARTER * (u + 1))
            nc.vector.quantize_mx(
                out=h_codes[a, half][:, cols].bitcast(FP8X4), scales=h_plane[a, half][:, cols], in_=woven[a, half, u][:]
            )

        y_acc = {}

        def output_pass(kind, i, m, half, start=False, stop=False):
            if start:
                y_acc[m, half] = bank(4 * half + m, "y_acc")
            first = N * i + P * m
            if kind == "skip":
                weights = ws_codes[:, 4 * first : 4 * (first + P)].bitcast(FP8X4)
                weight_plane = ws_plane[:, first : first + P]
                codes, plane = v_operand(i, half)
            else:
                weights = w2_codes[:, 2 * first : 2 * (first + P)].bitcast(FP4X4)
                weight_plane = w2_plane[:, first : first + P]
                codes, plane = h_codes[i, half][:].bitcast(FP8X4), h_plane[i, half][:]
            nc.tensor.matmul_mx(
                out=y_acc[m, half][:],
                lhsT=weights,
                lhsT_scale=weight_plane,
                rhs=codes,
                rhs_scale=plane,
                start=start,
                stop=stop,
            )

        def finish(m, half, pieces=1):
            width = HALF // pieces
            for i in range(pieces):
                result = sb("result%d%d%d" % (m, half, i), [P, width], F32)
                cols = slice(HALF * half + width * i, HALF * half + width * (i + 1))
                nc.vector.scalar_tensor_tensor(
                    out=result[:],
                    in0=y_acc[m, half][:, width * i : width * (i + 1)],
                    scalar=b2_cols[:, m : m + 1],
                    in1=edge_weight[:, cols],
                    op0=ALU.add,
                    op1=ALU.mult,
                )
                nc.sync.dma_start(out=out[P * m : P * (m + 1), cols], in_=result[:])
            return result

        for half in range(2):
            gather_words(HALF * half, HALF)

        unread = bank(5, "unread")
        for i in range(WARM_UPS):
            moving = picked[0][:, 0:QUARTER] if i == 0 else picked_scales[:]
            nc.tensor.matmul_mx(
                out=unread[:],
                lhsT=warm_codes[:].bitcast(FP8X4),
                lhsT_scale=warm_plane[:],
                rhs=moving.bitcast(FP4X4),
                rhs_scale=picked_scales[:, 0:HALF],
                start=i == 0,
                stop=i == WARM_UPS - 1,
            )

        for g in range(2):
            for half in range(2):
                part_words(half, g)
        stage(0, 0, 0, AT_STAIRS)
        round_w1(nc.scalar, 0, 0, 0)
        stage(0, 0, 1, AT_FIRST_SLOT)
        round_w1(nc.vector, 0, 0, 1, 0, FIRST_SHARE)
        round_w1(nc.scalar, 0, 0, 1, FIRST_SHARE, P)
        for u in range(2):
            quantize_w1(0, 0, u)
        stage(0, 1, 0, AT_STAIRS + KIB)
        round_w1(nc.vector, 0, 1, 0)
        stage(0, 1, 1, AT_SLOT_B)
        round_w1(nc.scalar, 0, 1, 1)
        for u in range(2):
            quantize_w1(0, 1, u)

        load_w1(1, 0, AT_RAW10)
        load_w1(1, 1, AT_RAW11)
        ws_codes = at(AT_WS, "ws_codes", [P, 2 * 4 * N], U8)
        nc.sync.dma_start(
            out=ws_codes[:].bitcast(I32).rearrange("p (a n) -> p a n", a=2),
            in_=ws_words.rearrange("a p n t -> p a (n t)").bitcast(I32),
        )
        load_weight_scales(ws_plane, ws_scales)
        w2_codes = at(AT_W2, "w2_codes", [P, 2 * 2 * N], U8)
        nc.sync.dma_start(
            out=w2_codes[:].bitcast(I32).rearrange("p (a n) -> p a n", a=2),
            in_=w2_words.rearrange("a p n -> p a n").bitcast(I32),
        )
        load_weight_scales(w2_plane, w2_scales)

        b2_cols = at(AT_RAW00, "b2_cols", [P, 4], F32)
        with nc.allow_non_contiguous_dma(reason="one bias value for each partition and row tile"):
            nc.sync.dma_start(out=b2_cols[:], in_=b2.rearrange("(m p) -> p m", p=P))

        for half in range(2):
            for t in range(2):
                first_layer(0, half, t, 0, False)
        first_layer(0, 0, 2, 0, False)
        for t in range(3):
            first_layer(0, 0, t, 1, True)
        for g in (1, 0):
            first_layer(0, 0, 3, g, g == 0)
        empty_banks(0, 0)
        for t in range(2):
            first_layer(0, 1, t, 1, True)
        for t in (2, 3):
            for g in (1, 0):
                first_layer(0, 1, t, g, g == 0)
        empty_banks(0, 1)

        for u, offset in enumerate((AT_STAIRS + 2 * KIB, AT_SLOT_B)):
            stage(1, 0, u, offset)
            round_w1(nc.vector, 1, 0, u)
        for u in range(2):
            quantize_w1(1, 0, u)
        stage(1, 1, 0, AT_STAIRS + 3 * KIB)
        round_w1(nc.vector, 1, 1, 0)
        stage(1, 1, 1, AT_SLOT_B)
        round_w1(nc.vector, 1, 1, 1, 0, P // 2)
        quantize_w1(1, 1, 0)
        round_w1(nc.vector, 1, 1, 1, P // 2, P)
        weave_h(0, 0, 0, nc.vector, AT_STAIRS + 2 * KIB)
        quantize_w1(1, 1, 1)
        for t in range(4):
            first_layer(1, 0, t, 0, False)
        for t in range(FILLERS):
            first_layer(1, 1, t, 0, False)
        for half in range(2):
            for t in range(2):
                first_layer(1, half, t, 1, True)
        for t in (2, 3):
            first_layer(1, 0, t, 1, True)
        for t in (2, 3):
            for g in (1, 0):
                first_layer(1, 1, t, g, g == 0)
        for half in range(2):
            empty_banks(1, half)

        weave_h(0, 0, 1, nc.vector, AT_STAIRS + 4 * KIB)
        for u in range(2):
            quantize_h(0, 0, u)
        for u in range(2):
            weave_h(0, 1, u, nc.vector, AT_STAIRS + (2 + 2 * u) * KIB)
        for u in range(2):
            weave_h(1, 0, u, nc.vector, AT_LATE_SLOTS[u])
        for u in range(2):
            quantize_h(1, 0, u)
        for u in range(2):
            quantize_h(0, 1, u, AT_LATE_SLOTS[0])
        for u in range(2):
            weave_h(1, 1, u, nc.scalar)
            quantize_h(1, 1, u)

        for m in range(4):
            for g in range(2):
                output_pass("skip", g, m, 0, start=g == 0)
        for a in range(2):
            for m in range(4):
                output_pass("layer", a, m, 0, stop=a == 1)
        for m in range(4):
            finish(m, 0)

        opening = (("layer", 0), ("skip", 0), ("skip", 1))

        def open_tile(m):
            for i, (kind, index) in enumerate(opening[::-1] if m == 0 else opening):
                output_pass(kind, index, m, 1, start=i == 0)

        def close_tile(m):
            output_pass("layer", 1, m, 1, stop=True)
            finish(m, 1, 2 if m == 3 else 1)

        for m in range(2):
            open_tile(m)
        for m in range(2):
            close_tile(m)
        for m in (2, 3):
            open_tile(m)
            close_tile(m)
